import numpy as np, ml_dtypes
CORES = [9,25,41,57]
N = 4
import mx_ref
BF = ml_dtypes.bfloat16
def gentries(a):
    return np.ascontiguousarray(a.reshape(8, 16, -1).transpose(0, 2, 1)).reshape(8, -1)
def gtable(e):
    e = np.asarray(e); return np.ascontiguousarray(e.reshape(8, -1, 16).transpose(0, 2, 1)).reshape(128, -1).astype(np.int32)
def gcols(t, e):
    v = np.concatenate([t.reshape(8, 16, -1, 4), np.zeros((8, 16, 1, 4), BF)], axis=2)
    return np.ascontiguousarray(np.stack([v[g][:, e[g]] for g in range(8)])).reshape(128, -1)
def gpick(z, e):
    return np.concatenate([z[16 * g:16 * g + 16][:, e[g]] for g in range(8)])
def tile(rs):
    return np.stack(rs, axis=2).reshape(128, -1).astype(BF)
def pick(q, e):
    c = np.concatenate([q[0].reshape(128, -1, 4), np.zeros((128, 1, 4), np.uint8)], axis=1); s = np.concatenate([q[1], np.ones((16, 1), np.uint8)], axis=1)
    return (np.ascontiguousarray(c[:, e].reshape(128, -1)), np.ascontiguousarray(s[:, e]))
def join(*qs):
    return (np.concatenate([q[0] for q in qs], axis=1), np.concatenate([q[1] for q in qs], axis=1))
def put(q, e, v):
    c, s = q[0].reshape(128, -1, 4).copy(), q[1].copy(); c[:, e] = v[0].reshape(128, -1, 4); s[:, e] = v[1]
    return (c.reshape(128, -1), s)
def pk(c, s):
    return (np.ascontiguousarray(c), mx_ref.live(s))
def emit(q):
    return q[0], q[1]
def packed(v, rng):
    q = [mx_ref.quantize(np.ascontiguousarray(v[r])) for r in range(N)]
    return np.stack([a for a, b in q]), np.stack([mx_ref.plane(b, rng) for a, b in q])
def values_of_codes():
    e, c = np.zeros((128, 128, 4), np.float32), np.zeros((128, 2, 4), np.uint8)
    e[np.arange(128), np.arange(128), 0] = 1
    c[:127, :, 0] = np.arange(256).reshape(2, 128).T[:127]
    return mx_ref.matmul(mx_ref.quantize(e.reshape(128, 512).astype(BF)), (c.reshape(128, 8), np.full((16, 2), 127, np.uint8))).T.reshape(-1).astype(np.float64)
CODE_VALUE, SCALE_VALUE = values_of_codes(), 2.0 ** (np.arange(256) - 127.0)
def decode(q):
    return (CODE_VALUE[q[0]].reshape(16, 8, -1, 4) * SCALE_VALUE[q[1]][:, None, :, None] + 0.0).reshape(128, -1).astype(np.float32)
def f(rng, *shape):
    return mx_ref.flush((rng.standard_normal(shape, dtype=np.float32) * np.exp2(rng.integers(-2, 3, shape[:-1] + (1,)))).astype(BF))
def wide(rng, *shape, cols=0):
    v = rng.standard_normal(shape, dtype=np.float32) * np.exp2(rng.integers(-12, 13, shape)).astype(np.float32)
    if cols: v *= np.repeat(np.exp2(rng.integers(-cols, cols + 1, shape[:-2] + (1, shape[-1] // 4))) * (rng.random(shape[:-2] + (1, shape[-1] // 4)) > 0.0625), 4, axis=-1).astype(np.float32)
    return mx_ref.flush(v.astype(BF))
C, R = 448, 3
DECIDE = [0, 1, 2, 16, 32, 48, 64, 80, 96, 112]
def big(a):
    a = a.astype(np.float32)
    a[np.abs(a) < np.float32(2.0 ** -16)] = 0
    return a
def numbers_of(rng):
    return big(f(rng, N, 128, 4 * C)).reshape(N, 8, 16, C, 4), f(rng, N, 128, 512).astype(np.float32).reshape(N, 8, 16, 128, 4), f(rng, N, 128, 512).astype(np.float32).reshape(N, 8, 16, 128, 4)
def layers(rng, still=[]):
    w = np.clip(big(f(rng, N, 128, 2048)), -1, 1).reshape(N, 8, 16, 4, 8, 16, 4)
    w[:, :, still] = 0
    w[:, :, :, :, :, still] = 0
    return w
def inputs(rng, x, u, v, p, w):
    x, u, v, w = [np.ascontiguousarray(a).astype(np.float32).reshape(N, 128, -1).astype(BF) for a in (x, u, v, w)]
    c, s = packed(w, rng)
    return {"x": x, "u": u, "v": v, "p": np.stack([gtable(p[r]) for r in range(N)]), "wc": c, "ws": s}
def pointers(rng):
    return rng.integers(0, C, (N, 8, C))
def setup_inputs(rng):
    x, u, v = numbers_of(rng)
    return inputs(rng, x, u, v, pointers(rng), layers(rng))
def setup_inputs_ties(rng):
    x, u, v = numbers_of(rng)
    o = rng.permutation(N)
    k = rng.integers(0, 3, (N, 8, C, 4))
    k[:, :, :, 2] -= 1
    k[:, :, :, 3] = 0
    k[o[1], :, :, 2] = 1
    x[:, :, 0] = k
    h = np.ones(N)
    h[o[0]] = 0
    h[o[1]] = -1
    u[:, :, :, DECIDE] = 0
    for g in range(8): u[:, g, 0, 16 * g, 0] = h
    u[:, 0, 0, 1, 1] = 1
    u[:, 0, 0, 2, 2] = 1
    u[o[2], :, :, 1] = 0
    u[o[3], :, :, 2] = 0
    return inputs(rng, x, u, v, pointers(rng), layers(rng, [0]))
def setup_inputs_near(rng):
    x, u, v = numbers_of(rng)
    hold = [0, 1] + [i for i in range(8, 16)]
    x[:, :, hold] = 0
    u[:, :, :, DECIDE] = 0
    o = rng.permutation(N) % 4
    e = 2.0 ** -30
    for r in range(N):
        k = 1.0 if o[r] == 0 else e
        s, n = rng.integers(0, 16, (8, C)), rng.integers(0, 16, C)
        c, m = rng.integers(0, 2, C) * 2.0 - 1.0, rng.integers(0, 2, C) * 2.0 - 1.0
        z = rng.integers(-1, 2, C)
        x[r, :, 8] = ((s[:, :, None] >> np.arange(4)) & 1) * np.exp2(np.arange(4) - 23.0)
        x[r, 0, 9] = ((n[:, None] >> np.arange(4)) & 1) * np.exp2(np.arange(4) - 23.0)
        if o[r] < 2:
            x[r, :, 0, :, 0] = c
            x[r, :, 11, :, 0] = 2.0 ** -10
            x[r, 0, 1, :, 0] = m
            x[r, 0, 12, :, 0] = 2.0 ** -10
            x[r, 1, 9, :, 0] = z * 2.0 ** -23
            u[r, 0, 1, 1, 0] = k
            u[r, 0, 12, 1, 0] = k
            u[r, 1, 9, 2, 0] = k
        elif o[r] == 2:
            x[r, :, 0, :, 0] = np.where(c < 0, -1.0, 0.0)
            x[r, 0, 1, :, 0] = np.where(rng.permutation(C) % 8 == 0, m, 0.0)
            x[r, 1, 13, :, 0] = z * e
            u[r, 0, 1, 1, 0] = 1
            u[r, 1, 13, 2, 0] = e
        else:
            x[r, :, 10, :, 0] = rng.integers(1, 3, (8, C)) * c * np.where(np.arange(8) < 4, e, 1.125 * e)[:, None]
            x[r, 0, 14, :, 0] = rng.integers(-2, 3, C) * e
            x[r, 1, 13, :, 0] = z * 1.125 * e
            x[r, 1, 14, :, 0] = (0 - z) * 1.25 * e
            u[r, 0, 14, 1, 0] = e
            u[r, 1, 13, 2, 0] = 1.125 * e
            u[r, 1, 14, 2, 0] = e
        if o[r] < 3: u[r, 0, 9, 1] = k
        far = rng.permutation(8)
        for g in range(8):
            if o[r] < 2:
                u[r, g, 0, 16 * g, 0] = k
                u[r, g, 11, 16 * g, 0] = k
            if o[r] == 2 and g in far[:2]: u[r, g, 0, 16 * g, 0] = 1
            if o[r] < 3: u[r, g, 8, 16 * g] = k
            else: u[r, g, 10, 16 * g, 0] = 1.25 * e if g < 4 else 1.125 * e
    return inputs(rng, x, u, v, pointers(rng), layers(rng, hold))
def setup_inputs_late(rng):
    x, u, v = numbers_of(rng)
    x[:, :, 0] = (rng.permutation(N) % 2 * 0.0625)[:, None, None, None]
    u[:, :, :, DECIDE] = 0
    for g in range(8): u[:, g, 0, 16 * g, 0] = 1
    u[:, 0, 0, 1, 1] = 1
    u[:, 0, 0, 2, 2] = 1
    return inputs(rng, x, u, v, pointers(rng), layers(rng))
def setup_inputs_ends(rng):
    x, u, v = numbers_of(rng)
    o, h = rng.permutation(N), rng.permutation(8)
    p = pointers(rng)
    x[:] = np.where(rng.random((N, 8, 1, C, 1)) < 0.5, 0.875, 1.0) * 2.0 ** 25
    v[:] = (rng.integers(0, 2, (N, 1, 1, 128, 1)) * 2.0 - 1.0) * 2.0 ** 30
    u[:, :, :, DECIDE] = 2.0 ** 30
    for g in range(8): u[:, g, :, 16 * g] = 2.0 ** 29
    u[:, :, :, 2] = 0
    u[:, 0, :, 2] = 2.0 ** 30
    u[:, 1, :, 2] = -2.0 ** 30
    p[o[0]] = C - 1
    x[o[0], :, :, :C - 1] = 2.0 ** -30
    u[o[0], :, :, 2] = -2.0 ** 30
    p[o[1]] = 0
    x[o[1]] = 2.0 ** 25
    u[o[1], :, :, ::16] = 2.0 ** 30
    u[o[1], :, :, 2] = 2.0 ** 30
    p[o[2], h[:4]] = C - 1
    p[o[2], h[4:]] = 0
    p[o[2], 0] = rng.permutation(C)
    x[o[2], :, :, 1 + rng.permutation(C - 2)[:C // 2]] = 2.0 ** -30
    u[o[2], :, :, ::16] = -2.0 ** 30
    u[o[2], 0, :, 112] = -2.0 ** 29
    u[o[2], :, :, 1] *= -1
    u[o[2], :, :, 2] = 2.0 ** 30
    for g in h[:4]: u[o[3], :, :, 16 * g] *= -1
    u[o[3], :, :, 3:16] = 2.0 ** -30
    v[o[3]] = 2.0 ** -30
    return inputs(rng, x, u, v, p, np.ones((N, 128, 2048)))
def setup_inputs_spread(rng):
    x, u, v = numbers_of(rng)
    return inputs(rng, big(wide(rng, N, 128, 4 * C, cols=6)), u, v, pointers(rng), layers(rng))
def check_inputs(d):
    b = []
    for k, top in (("x", 2.0 ** 25), ("u", 2.0 ** 30), ("v", 2.0 ** 30)):
        a = np.abs(d[k].astype(np.float32))
        if not (np.isfinite(a).all() and ((a == 0) | (a >= 2.0 ** -30) & (a <= top)).all()): b.append("a value of " + k)
    if not ((d["p"] >= 0) & (d["p"] < C)).all(): b.append("an entry of p")
    none, least, most = [emit(mx_ref.quantize(np.full((128, 16), k, np.float32).astype(BF)))[1][0, 0] for k in (0.0, 2.0 ** -30, 1.0)]
    for r in range(N):
        if ((d["wc"][r] == 0x7F) | (d["wc"][r] == 0xFF)).any(): b.append("wc: a code that is no number")
        s = mx_ref.live(d["ws"][r])
        if ((s != none) & ((s < least) | (s > most))).any(): b.append("ws: a scale out of range")
        with np.errstate(all="ignore"):
            if not (np.abs(decode(pk(d["wc"][r], d["ws"][r]))) <= 1).all(): b.append("a number of W beyond 1 in size")
    return b
def reference(x, u, v, p, wc, ws):
    qu = [mx_ref.quantize(u[r]) for r in range(N)]
    lay = [pk(wc[r], ws[r]) for r in range(N)]
    first = np.stack([gentries(p[r]) for r in range(N)])
    ptr = first.copy()
    now = [x[r] for r in range(N)]
    g, j = np.arange(8)[:, None], np.arange(C)
    for t in range(R):
        sent, via = [], []
        for r in range(N):
            s = mx_ref.matmul(qu[r], mx_ref.quantize(now[r])) + np.float32(0.0)
            level = np.argmax(s[::16], axis=0)
            o = np.argsort(-s[1], kind="stable")
            c = np.zeros(C, np.int64)
            c[o] = np.roll(o, -1)
            call = s[2] > 0
            new = np.where((g < level) & call, ptr[r][:, c], ptr[r])
            new = np.where(g == level, np.where(call, j, first[r]), new)
            ptr[r] = new
            via.append(new[:, c])
            sent.append(mx_ref.quantize(gcols(now[r], new)))
        for r in range(N):
            q = sent[(r - 1 - t) % N]
            h = [mx_ref.matmul(pick(lay[r], np.arange(128 * b, 128 * b + 128)), q) * np.float32(0.00390625) for b in range(4)]
            now[r] = tile([gpick(h[b], via[r]) + now[r][:, b::4].astype(np.float32) for b in range(4)])
    y, op = np.zeros((N, 128, C), np.float32), np.zeros((N, 8, C), np.float32)
    oc, osc = np.zeros((N, 128, 4 * C), np.uint8), np.zeros((N, 16, C), np.uint8)
    for r in range(N):
        q = mx_ref.quantize(now[r])
        y[r] = mx_ref.matmul(mx_ref.quantize(v[r]), q)
        op[r] = ptr[r]
        oc[r], osc[r] = emit(q)
    return {"y": y, "op": op, "oc": oc, "osc": osc}

@@ -1,0 +1,415 @@
+from concourse.mybir import dt, AluOpType as A, ActivationFunctionType as F
+
+C, R, N = 448, 3, 4
+H = [(0, 256), (256, 448)]
+HZ = [(0, 224), (224, 448)]
+BIG = -1.0e29
+NIL = 448
+
+
+def _b(n, t="float32"):
+    return ("sbuf", [128, n], t)
+
+
+BF, CODE, U8, U16, I32 = "bfloat16", "float8_e4m3fn_x4", "uint8", "uint16", "int32"
+SCRATCH = {
+    "PS": ("psum", [128, 4096], "float32"),
+    "UT": _b(512, BF), "VT": _b(512, BF), "ZT": _b(512, BF), "Z": _b(1792, BF), "THR": _b(128, BF),
+    "SG": _b(1792, BF), "CM": _b(1792, BF), "SCN": _b(1792, BF),
+    "QU": _b(128, CODE), "QUS": _b(128, U8), "QU1": _b(128, CODE), "QU1S": _b(128, U8), "QV": _b(128, CODE), "QVS": _b(128, U8),
+    "WC": _b(512, CODE), "WS": _b(512, U8), "QX": _b(512, CODE), "QXS": _b(512, U8),
+    "PI": _b(28, I32), "PIX": _b(1, I32), "PMI": _b(1, I32), "GI": _b(1, I32),
+    "DUP0": _b(2, U16), "DUP1": _b(2, U16), "U1L": _b(8, U16),
+    "PM": _b(1), "PF": _b(1), "NG": _b(1), "NG16": _b(1), "GQ": _b(1), "WQ": _b(1), "PD": _b(456), "IO4": _b(1792), "MD": _b(448), "MASK": _b(448),
+    "A16": _b(28), "Z8": _b(8), "NS": _b(4), "RUN": _b(32), "LJ": _b(32), "LV": _b(4), "CF": _b(4),
+    "NAT": _b(32), "TT": _b(32), "LT0": _b(32), "LT1": _b(32), "LR": _b(64), "RM": _b(448), "SC": _b(232), "SCa": _b(120), "SCb": _b(120), "YS": _b(448),
+}
+for _i in ("EL", "RK", "RK1", "OL", "OF0", "OF1", "OF2", "OF3"):
+    SCRATCH[_i] = _b(28, U16)
+for _i in ("JW", "PW", "JP", "JD", "PDF", "KK", "Q", "wf", "lm", "mq", "a1", "a2", "al", "b1", "b2", "m1", "m2", "m3", "k1", "k2", "k3", "dc", "ED", "D1", "D2", "D3"):
+    SCRATCH[_i] = _b(28)
+for _i in range(4):
+    SCRATCH["X%d" % _i] = _b(1792, BF)
+    SCRATCH["HS%d" % _i] = _b(448)
+    SCRATCH["DR%d" % _i] = _b(448)
+for _i in range(R):
+    for _n in ("QZ", "LZ"):
+        SCRATCH["%s%d" % (_n, _i)] = _b(448, CODE)
+        SCRATCH["%sS%d" % (_n, _i)] = _b(448, U8)
+
+SEMAPHORES = ["sv", "ss", "st", "sg", "loc"]
+SEMAPHORES += ["ld%d" % _i for _i in range(8)] + ["sto%d" % _i for _i in range(12)]
+SEMAPHORES += ["ar%d%d%s" % (_t, _h, _k) for _t in range(R) for _h in range(2) for _k in "cs"]
+
+
+def rank_program(g, core, T, topo):
+    rank = T.rank_of(core)
+    if rank is None:
+        return
+    q = {"v": g.vector, "s": g.scalar, "t": g.tensor, "g": g, "y": g.sync}
+    own = {"v": "sv", "s": "ss", "t": "st", "g": "sg"}
+    cnt, known, clock, lastw, readers = {}, {k: {} for k in q}, {}, {}, {}
+
+    def waits(qn, reads, writes):
+        need = {}
+        for k in reads:
+            if k in lastw:
+                s, n, _ = lastw[k]
+                need[s] = max(need.get(s, 0), n)
+        for k in writes:
+            if k in lastw:
+                s, n, _ = lastw[k]
+                need[s] = max(need.get(s, 0), n)
+            for s, n, rq in readers.get(k, []):
+                if rq != qn:
+                    need[s] = max(need.get(s, 0), n)
+        kn = known[qn]
+        need = {s: n for s, n in need.items() if kn.get(s, 0) < n}
+        for s in list(need):
+            if any(o != s and clock.get((o, need[o]), {}).get(s, 0) >= need[s] for o in need):
+                del need[s]
+        for s, n in need.items():
+            q[qn].wait_ge(T.sem[s], n)
+            for o, m in clock.get((s, n), {}).items():
+                kn[o] = max(kn.get(o, 0), m)
+            kn[s] = max(kn.get(s, 0), n)
+
+    def note(qn, reads, writes, s, n, dma):
+        clock[(s, n)] = dict(known[qn])
+        for k in writes:
+            lastw[k] = (s, n, qn)
+            readers[k] = []
+        for k in reads:
+            readers.setdefault(k, []).append((s, n, None if dma else qn))
+
+    def do(qn, fn, args, reads, writes, **kw):
+        waits(qn, reads, writes)
+        s = own[qn]
+        n = cnt.get(s, 0) + 1
+        cnt[s] = n
+        fn(*args, **kw).then_inc(T.sem[s], 1)
+        note(qn, reads, writes, s, n, False)
+
+    def dma(qn, s, out, in_, reads, writes):
+        waits(qn, reads, writes)
+        q[qn].dma_start(out, in_).then_inc(T.sem[s], 16)
+        cnt[s] = 16
+        note(qn, reads, writes, s, 16, True)
+
+    V, S, TE = g.vector, g.scalar, g.tensor
+
+    def ts(out, in0, s1, s2, ops, reads, writes):
+        do("v", V.tensor_scalar, (out, in0, s1, s2) + tuple(ops), reads, writes)
+
+    def tt(out, a, b, op, reads, writes):
+        do("v", V.tensor_tensor, (out, a, b, op), reads, writes)
+
+    def vcopy(out, a, reads, writes):
+        do("v", V.tensor_copy, (out, a), reads, writes)
+
+    def act(out, a, f, reads, writes, **kw):
+        do("s", S.activation, (out, a, f), reads, writes, **kw)
+
+    def scan(out, a, b, init, o0, o1, reads, writes):
+        do("v", V.tensor_tensor_scan, (out, a, b, init, o0, o1), reads, writes)
+
+    def quant(oc, os_, tile, reads, writes):
+        do("v", V.quantize_mx, (oc, os_, tile), reads, writes)
+
+    def mm(bank, n, l, ls, r, rs, reads):
+        do("t", TE.matmul_mx, (T.PS[:, 512 * bank:512 * bank + n], l, ls, r, rs, True, True), reads, ["bk%d" % bank])
+
+    def fill(ap, c, key):
+        do("v", V.memset, (ap, c), [], [key])
+
+    def iota(out, pattern, key, mult=0, flag=True):
+        kw = {"allow_small_or_imprecise_dtypes": True} if flag else {}
+        do("g", g.iota, (out, pattern, 0, mult), [], [key], **kw)
+
+    dma("y", "ld0", T.X0[:, 0:1024], T.x[:, 0:1024], [], ["X0h0"])
+    dma("s", "ld1", T.UT[:, :], T.u[:, :], [], ["UT"])
+    dma("s", "ld2", T.PI[:, :], T.p[:, :], [], ["PI"])
+    dma("y", "ld3", T.X0[:, 1024:1792], T.x[:, 1024:1792], [], ["X0h1"])
+    dma("y", "ld4", T.WC[:, :].bitcast(dt.uint8), T.wc[:, :], [], ["WC"])
+    dma("y", "ld5", T.WS[:, :], T.ws[:, :], [], ["WS"])
+    dma("y", "ld6", T.VT[:, :], T.v[:, :], [], ["VT"])
+
+    iota(T.PIX[:, :], [[0, 1]], "PIX", 1, False)
+    iota(T.A16[:, :], [[16, 28]], "A16")
+    iota(T.MD[:, :], [[0, 28], [1, 16]], "MD")
+    iota(T.IO4[:, :], [[1, 448], [0, 4]], "IO4")
+    fill(T.U1L[:, :], 1, "U1L")
+    fill(T.ZT[:, :], 0.0, "ZT")
+    fill(T.Z8[:, :], 0.0, "Z8")
+    fill(T.SC[:, :], 0.0, "SC")
+    fill(T.SCa[:, :], 0.0, "SCa")
+    fill(T.SCb[:, :], 0.0, "SCb")
+    fill(T.PD[:, NIL:456], 0.0, "PDz")
+    fill(T.TT[:, :], 0.0, "TT")
+    quant(T.QX[:, 384:512], T.QXS[:, 384:512], T.ZT[:, :], ["ZT"], ["QXh1", "QXz"])
+    ts(T.PMI[:, :], T.PIX[:, :], 15, None, [A.bitwise_and], ["PIX"], ["PMI"])
+    ts(T.GI[:, :], T.PIX[:, :], 4, None, [A.arith_shift_right], ["PIX"], ["GI"])
+    vcopy(T.PF[:, :], T.PIX[:, :], ["PIX"], ["PF"])
+    vcopy(T.PM[:, :], T.PMI[:, :], ["PMI"], ["PM"])
+    ts(T.NG[:, :], T.GI[:, :], -1.0, -225.0, [A.mult, A.add], ["GI"], ["NG"])
+    ts(T.NG16[:, :], T.GI[:, :], -1.0, -241.0, [A.mult, A.add], ["GI"], ["NG16"])
+    ts(T.GQ[:, :], T.GI[:, :], 448.0, 448.0 * 242, [A.mult, A.add], ["GI"], ["GQ"])
+    fill(T.WQ[:, :], -448.0 * 447, "WQ")
+    for e in range(2):
+        ts(T["DUP%d" % e][:, :], T.Z8[:, 0:2], T.PM[:, 0:1], 16.0 * e, [A.add, A.add], ["Z8", "PM"], ["DUP%d" % e])
+    ts(T.JW[:, :], T.A16[:, :], T.PM[:, 0:1], None, [A.add], ["A16", "PM"], ["JW"])
+
+    quant(T.QU[:, :], T.QUS[:, :], T.UT[:, :], ["UT"], ["QU"])
+    vcopy(T.QU1[:, :].bitcast(dt.uint32), T.QU[:, 0:128].bitcast(dt.uint32).indirect(T.U1L[:, 0:8]), ["QU", "U1L"], ["QU1c"])
+    act(T.QU1S[:, :], T.QUS[:, 0:128].indirect(T.U1L[:, 0:8]), F.Copy, ["QU", "U1L"], ["QU1s"])
+
+    def quant_x(t, h):
+        a, b = H[h]
+        quant(T.QX[:, a:b], T.QXS[:, a:b], T["X%d" % t][:, 4 * a:4 * b], ["X%dh%d" % (t, h)], ["QXh%d" % h])
+
+    def products(h):
+        a, b = H[h]
+        for m in (0, 1) if h == 0 else (2, 3):
+            mm(m, 128, T.QX[:, 128 * m:128 * m + 128], T.QXS[:, 128 * m:128 * m + 128], T.QU[:, :], T.QUS[:, :],
+               ["QXh%d" % h, "QU"] + (["QXz"] if m == 3 else []))
+        mm(4 + h, b - a, T.QU1[:, :], T.QU1S[:, :], T.QX[:, a:b], T.QXS[:, a:b], ["QXh%d" % h, "QU1c", "QU1s"])
+
+    def negs(m):
+        act(T.NS[:, m:m + 1], T.PS[:, 512 * m + 1:512 * m + 2], F.Copy, ["bk%d" % m], ["NS%d" % m], scale=-1.0)
+
+    def sign(m, h):
+        a, b = H[h]
+        act(T.SG[:, 448 * m + a:448 * m + b], T.PS[:, 512 * (4 + h):512 * (4 + h) + b - a], F.Sign,
+            ["bk%d" % (4 + h), "NS%d" % m], ["SG%d%d" % (m, h)], bias=T.NS[:, m:m + 1])
+
+    def runmax(m):
+        scan(T.RUN[:, 8 * m:8 * m + 8], T.Z8[:, :], T.PS[:, 512 * m:512 * m + 128:16], BIG, A.add, A.max, ["Z8", "bk%d" % m, "NS%d" % m], ["RUN%d" % m])
+
+    def level(m):
+        act(T.LJ[:, 8 * m:8 * m + 8], T.RUN[:, 8 * m:8 * m + 8], F.Sign, ["RUN%d" % m], ["LJ%d" % m, "LV%d" % m],
+            bias=T.RUN[:, 8 * m + 7:8 * m + 8], scale=-1.0, accum_out=T.LV[:, m:m + 1])
+
+    def before(m, a, b, kind):
+        o = 448 * m
+        rd = ["SG%d%d" % (m, h) for h in (0, 1) if a < H[h][1] and b > H[h][0]]
+        if kind == "tri":
+            tt(T.CM[:, o + a:o + b], T.SG[:, o + a:o + b], T.THR[:, 0:b - a], A.is_gt, rd + ["THR"], ["CM%d.%d" % (m, a)])
+        else:
+            ts(T.CM[:, o + a:o + b], T.SG[:, o + a:o + b], 0.0, None, [kind], rd, ["CM%d.%d" % (m, a)])
+
+    def count(m, parts):
+        o = 448 * m
+        scan(T.SCN[:, 224 * m:224 * m + 224], T.CM[:, o:o + 224], T.CM[:, o + 224:o + 448], -225.0, A.add, A.add,
+             ["CM%d.%d" % (m, a) for a in parts], ["SCN%d" % m])
+
+    def vv(o, a, b, op):
+        tt(T[o][:, 0:28], T[a][:, 0:28], T[b][:, 0:28], op, (LRK if a == "LR" else [a]) + [b], [o])
+
+    def prep(t, o):
+        vv(o, {"JD": "JW", "PDF": "PW", "KK": "JP"}[o], "D%d" % t if t else "PW", A.subtract)
+
+    def scores_head():
+        negs(0); negs(1)
+        sign(0, 0); sign(1, 0)
+
+    def scores_tail():
+        level(0); level(1)
+        negs(2); negs(3)
+        sign(2, 0); sign(3, 0)
+        for m in range(4):
+            sign(m, 1)
+        before(1, 0, 128, A.is_ge)
+        before(0, 0, 128, "tri")
+        before(1, 128, 256, "tri")
+        runmax(2); runmax(3)
+        level(2); level(3)
+        ts(T.CF[:, :], T.PS[:, 2:2048:512], 0.0, 16.0, [A.is_gt, A.mult], ["bk0", "bk1", "bk2", "bk3"], ["CF"])
+        before(2, 0, 256, A.is_ge)
+        before(3, 0, 256, A.is_ge)
+        before(0, 128, 448, A.is_gt)
+        before(1, 256, 448, A.is_gt)
+        count(0, [0, 128])
+        before(2, 256, 384, "tri")
+        count(1, [0, 128, 256])
+        before(2, 384, 448, A.is_gt)
+        before(3, 384, 448, "tri")
+        before(3, 256, 384, A.is_ge)
+        count(2, [0, 256, 384])
+        count(3, [0, 256, 384])
+        tt(T.SCN[:, 4 * 224 + 223:1792:224], T.LV[:, :], T.CF[:, :], A.add, ["LV0", "LV1", "LV2", "LV3", "CF"], ["SCNw"])
+
+    LRK = ["LRe0", "LRe1", "LR1", "LR2", "LR3"]
+    RKK = ["RK%d" % b for b in range(4)]
+
+    def lists(t):
+        rd = ["SCN0", "SCN1", "SCN2", "SCN3", "SCNw"]
+        prep(t, "JD")
+        for b in range(4):
+            ts(T.NAT[0:32, b:32:4], T.SCN[32 * b:32 * b + 32, 223:1792:224], 225.0, None, [A.add], rd, ["NAT%d" % b])
+        prep(t, "PDF")
+        do("v", V.transpose, (T.TT[0:32, 0:32], T.NAT[0:32, 0:32]), ["NAT%d" % b for b in range(4)], ["TT"])
+        prep(t, "KK")
+        for e in range(2):
+            vcopy(T["LT%d" % e][:, :], T.TT[:, 0:32].indirect(T["DUP%d" % e][:, 0:2]), ["TT", "DUP%d" % e], ["LT%d" % e])
+        for e in range(2):
+            do("v", V.transpose, (T.LR[0:32, e:64:2], T["LT%d" % e][0:32, 0:32]), ["LT%d" % e], ["LRe%d" % e])
+        for b in range(4):
+            ts(T.RK[32 * b:32 * b + 32, :], T.LR[0:32, 0:28], -1.0, None, [A.add], ["LRe0", "LRe1"], ["RK%d" % b])
+        for b in range(1, 4):
+            act(T.LR[32 * b:32 * b + 32, 0:64], T.LR[0:32, 0:64], F.Copy, ["LRe0", "LRe1"], ["LR%d" % b])
+
+    def sorted_row(t):
+        vcopy(T.PD[:, 0:448].indirect(T.RK[:, 0:28]), T["DR%d" % t][:, :], RKK + ["DR%d" % t], ["PD"])
+
+    def pointers(t):
+        k = "D%d" % t if t else "PW"
+        W = T.LR[:, 32:60]
+        sorted_row(t)
+        act(T.wf[:, :], T.LR[:, 0:28], F.Relu, LRK + ["WQ"], ["wf"], bias=T.WQ[:, 0:1], scale=448.0)
+        act(T.Q[:, :], W, F.Relu, LRK + ["GQ"], ["Q"], bias=T.GQ[:, 0:1], scale=-448.0)
+        act(T.a1[:, :], W, F.Sign, LRK + ["NG16"], ["a1"], bias=T.NG16[:, 0:1])
+        act(T.a2[:, :], W, F.Sign, LRK + ["NG"], ["a2"], bias=T.NG[:, 0:1])
+        act(T.b1[:, :], T.a1[:, :], F.Square, ["a1"], ["b1"])
+        act(T.b2[:, :], T.a2[:, :], F.Square, ["a2"], ["b2"])
+        act(T.al[:, :], T.a1[:, :], F.Relu, ["a1"], ["al"])
+        vv("lm", "LR", "wf", A.subtract)
+        vv("m1", "b1", "JD", A.mult)
+        vv("mq", "lm", "Q", A.max)
+        vv("m2", "b2", "PDF", A.mult)
+        ts(T.OL[:, :], T.mq[:, :], float(NIL), None, [A.min], ["mq"], ["OL"])
+        vv("m3", "al", k, A.mult)
+        tt(T.RM[:, :], T.PD[:, 0:456].indirect(T.OL[:, 0:28]), T.MASK[:, :], A.mult, ["PD", "PDz", "OL", "MASK"], ["RM"])
+        vv("k1", "KK", "m1", A.subtract)
+        scan(T.SC[:, 1:225], T.RM[:, 0:448:2], T.RM[:, 1:448:2], 0.0, A.add, A.add, ["RM"], ["SC"])
+        vv("k2", "m2", "m3", A.add)
+        tt(T.dc[:, :], T.SC[:, 8:225:8], T.SC[:, 0:217:8], A.subtract, ["SC"], ["dc"])
+        vv("k3", "k1", "k2", A.subtract)
+        vcopy(T.RK1[:, :], T.lm[:, :], ["lm"], ["RK1"])
+        n = "D%d" % (t + 1)
+        vv(n, "dc", "k3", A.add)
+        for e in (2, 0, 3, 1):
+            ts(T["OF%d" % e][:, :], T[n][:, :], 4.0, float(e), [A.mult, A.add], [n], ["OF%d" % e])
+
+    def send(t, h):
+        a, b = HZ[h]
+        dst = T.cores[(rank + 1 + t) % N]
+        rid, pid, _ = topo.addr(dst)
+        m = topo.mask(core, dst)
+        waits("g", ["QZ%dh%d" % (t, h)], [])
+        g.remote_dma(T["LZ%d" % t][:, a:b].bitcast(dt.uint8), T["QZ%d" % t][:, a:b].bitcast(dt.uint8),
+                     T.sem["ar%d%dc" % (t, h)], T.sem.loc, pid, rid, m)
+        g.remote_dma(T["LZS%d" % t][:, a:b], T["QZS%d" % t][:, a:b], T.sem["ar%d%ds" % (t, h)], T.sem.loc, pid, rid, m)
+        cnt["loc"] = cnt.get("loc", 0) + 2 * len(topo.engines(core, dst))
+        e = len(topo.engines(T.cores[(rank - 1 - t) % N], core))
+        lastw["LZ%dh%d" % (t, h)] = ("ar%d%dc" % (t, h), e, None)
+        lastw["LZS%dh%d" % (t, h)] = ("ar%d%ds" % (t, h), e, None)
+
+    def mosaic(t):
+        X = T["X%d" % t]
+
+        def part(h, e):
+            a, b = HZ[h]
+            o, i = T.Z[:, 4 * a + e:4 * b:4], X[:, 0:1792].indirect(T["OF%d" % e][:, a // 16:b // 16])
+            rd, wr = ["X%dh0" % t, "X%dh1" % t, "OF%d" % e], ["Zh%d.%d" % (h, e)]
+            if e >= 2:
+                act(o, i, F.Copy, rd, wr)
+            else:
+                vcopy(o, i, rd, wr)
+
+        def pack(h):
+            a, b = HZ[h]
+            quant(T["QZ%d" % t][:, a:b], T["QZS%d" % t][:, a:b], T.Z[:, 4 * a:4 * b],
+                  ["Zh%d.%d" % (h, e) for e in range(4)], ["QZ%dh%d" % (t, h)])
+            send(t, h)
+
+        for h in range(2):
+            part(h, 2); part(h, 3)
+        for h in range(2):
+            part(h, 0); part(h, 1)
+            pack(h)
+        act(T["DR%d" % (t + 1)][:, :], T.IO4[:, :].indirect(T.OF0[:, 0:28]), F.Copy, ["IO4", "OF0"], ["DR%d" % (t + 1)])
+
+    def join_list(t):
+        sorted_row(t + 1)
+        for h, s in enumerate("ab"):
+            tt(T.RM[:, 224 * h:224 * h + 224], T.PD[:, 0:456].indirect(T.RK1[:, 14 * h:14 * h + 14]), T.MASK[:, 224 * h:224 * h + 224], A.mult,
+               ["PD", "PDz", "RK1", "MASK", "RM"], ["RM" + s])
+        for h, s in enumerate("ab"):
+            o = 224 * h
+            scan(T["SC" + s][:, 1:113], T.RM[:, o:o + 224:2], T.RM[:, o + 1:o + 224:2], 0.0, A.add, A.add, ["RM" + s], ["SC" + s])
+        for h, s in enumerate("ab"):
+            tt(T.ED[:, 14 * h:14 * h + 14], T["SC" + s][:, 8:113:8], T["SC" + s][:, 0:105:8], A.subtract, ["SC" + s], ["ED" + s])
+        for h, s in enumerate("ab"):
+            vcopy(T.EL[:, 14 * h:14 * h + 14], T.ED[:, 14 * h:14 * h + 14], ["ED" + s], ["EL" + s])
+
+    def layer(t):
+        for h in range(2):
+            a, b = HZ[h]
+            for w in range(4):
+                mm(2 * w + h, b - a, T.WC[:, 128 * w:128 * w + 128], T.WS[:, 128 * w:128 * w + 128], T["LZ%d" % t][:, a:b], T["LZS%d" % t][:, a:b],
+                   ["WC", "WS", "LZ%dh%d" % (t, h), "LZS%dh%d" % (t, h)])
+        for w, h in ((0, 0), (1, 0), (0, 1), (2, 0), (1, 1), (3, 0), (2, 1), (3, 1)):
+            a, b = HZ[h]
+            bk = 2 * w + h
+            act(T["HS%d" % w][:, a:b], T.PS[:, 512 * bk:512 * bk + b - a], F.Copy, ["bk%d" % bk], ["HS%dh%d" % (w, h)], scale=0.00390625)
+
+    def join(t, h, ws=range(4)):
+        a, b = H[h]
+        for w in ws:
+            tt(T["X%d" % (t + 1)][:, 4 * a + w:4 * b:4], T["HS%d" % w][:, 0:448].indirect(T.EL[:, a // 16:b // 16]),
+               T["X%d" % t][:, 4 * a + w:4 * b:4], A.add, ["HS%dh0" % w, "HS%dh1" % w, "ELa", "ELb", "X%dh%d" % (t, h)], ["X%dh%d.%d" % (t + 1, h, w)])
+        lastw["X%dh%d" % (t + 1, h)] = lastw["X%dh%d.%d" % (t + 1, h, ws[-1])]
+
+    quant_x(0, 0)
+    products(0)
+    scores_head()
+    quant_x(0, 1)
+    products(1)
+    vcopy(T.PW[:, :], T.PI[:, :], ["PI"], ["PW"])
+    ts(T.OF0[:, :], T.PI[:, :], 4.0, None, [A.mult], ["PI"], ["OF0"])
+    runmax(0); runmax(1)
+    ts(T.MASK[:, :], T.MD[:, :], T.PM[:, 0:1], None, [A.is_equal], ["MD", "PM"], ["MASK"])
+    vv("JP", "JW", "PW", A.add)
+    ts(T.THR[:, :], T.IO4[:, 0:512:4], T.PF[:, 0:1], 0.5, [A.is_gt, A.subtract], ["IO4", "PF"], ["THR"])
+    scores_tail()
+    act(T.DR0[:, :], T.IO4[:, :].indirect(T.OF0[:, 0:28]), F.Copy, ["IO4", "OF0"], ["DR0"])
+
+    for t in range(R):
+        lists(t)
+        pointers(t)
+        mosaic(t)
+        join_list(t)
+        layer(t)
+        if t == 0:
+            quant(T.QV[:, :], T.QVS[:, :], T.VT[:, :], ["VT"], ["QV"])
+        join(t, 0)
+        if t < R - 1:
+            join(t, 1, [0])
+        quant_x(t + 1, 0)
+        if t < R - 1:
+            products(0)
+            scores_head()
+            join(t, 1, [1, 2])
+            runmax(0)
+            join(t, 1, [3])
+            runmax(1)
+            quant_x(t + 1, 1)
+            products(1)
+            scores_tail()
+    dma("y", "sto0", T.op[:, :], T.DR3[0:128:16, :], ["DR3"], ["op"])
+    dma("y", "sto1", T.oc[:, 0:1024], T.QX[:, 0:256].bitcast(dt.uint8), ["QXh0"], ["oc0"])
+    mm(6, 256, T.QV[:, :], T.QVS[:, :], T.QX[:, 0:256], T.QXS[:, 0:256], ["QV", "QXh0"])
+    act(T.YS[:, 0:256], T.PS[:, 3072:3328], F.Copy, ["bk6"], ["YS0"])
+    dma("y", "sto2", T.y[:, 0:256], T.YS[:, 0:256], ["YS0"], ["y0"])
+    join(R - 1, 1)
+    quant_x(R, 1)
+    mm(7, 192, T.QV[:, :], T.QVS[:, :], T.QX[:, 256:448], T.QXS[:, 256:448], ["QV", "QXh1"])
+    dma("y", "sto3", T.oc[:, 1024:1792], T.QX[:, 256:448].bitcast(dt.uint8), ["QXh1"], ["oc1"])
+    for k in range(4):
+        dma("s" if k % 2 else "y", "sto%d" % (5 + k), T.osc[4 * k:4 * k + 4, :], T.QXS[32 * k:32 * k + 4, 0:448], ["QXh0", "QXh1"], ["osc%d" % k])
+    vcopy(T.YS[:, 256:448], T.PS[:, 3584:3776], ["bk7"], ["YS1"])
+    dma("s", "sto4", T.y[:, 256:448], T.YS[:, 256:448], ["YS1"], ["y1"])
+    kn = known["g"]
+    for s in sorted(cnt):
+        if kn.get(s, 0) < cnt[s]:
+            g.wait_ge(T.sem[s], cnt[s])

@@ -1,10 +1,15 @@
 from concourse.mybir import dt, AluOpType as A, ActivationFunctionType as F
 
 C, R, N = 448, 3, 4
-H = [(0, 256), (256, 448)]
-HZ = [(0, 224), (224, 448)]
-BIG = -1.0e29
-NIL = 448
+MID = 224
+ZP = [(0, 128), (128, 288), (288, 448)]
+MOSAIC = [("pick", "v", 0, 128), ("pick", "s", 128, 288), ("pick", "s", 288, 448),
+          ("fold", 0, 128), ("four", 0, 128), ("part", "s", 48, 128), ("fold", 128, 288), ("part", "v", 0, 48), ("four", 128, 288),
+          ("part", "s", 184, 288), ("fold", 288, 448), ("pack", 0), ("four", 288, 448), ("part", "s", 360, 448), ("part", "v", 128, 184), ("pack", 1),
+          ("part", "v", 288, 360), ("pack", 2)]
+XL = [(0, 128), (128, 256), (256, 448)]
+BIG = 1.0e29
+TP, TI, TS = 4 * C, 5 * C, 6 * C
 
 
 def _b(n, t="float32"):
@@ -14,24 +19,25 @@ def _b(n, t="float32"):
 BF, CODE, U8, U16, I32 = "bfloat16", "float8_e4m3fn_x4", "uint8", "uint16", "int32"
 SCRATCH = {
     "PS": ("psum", [128, 4096], "float32"),
-    "UT": _b(512, BF), "VT": _b(512, BF), "ZT": _b(512, BF), "Z": _b(1792, BF), "THR": _b(128, BF),
-    "SG": _b(1792, BF), "CM": _b(1792, BF), "SCN": _b(1792, BF),
-    "QU": _b(128, CODE), "QUS": _b(128, U8), "QU1": _b(128, CODE), "QU1S": _b(128, U8), "QV": _b(128, CODE), "QVS": _b(128, U8),
+    "UT": _b(512, BF), "VT": _b(512, BF), "Z": _b(1792, BF), "THR": _b(128, BF),
+    "SG": _b(1792, BF), "CM": _b(1792, BF), "SCN": _b(1968, BF),
+    "TT": _b(32, BF), "LT0": _b(32, BF), "LT1": _b(32, BF), "LR": _b(64, BF),
+    "QU": _b(128, CODE), "QUS": _b(128, U8), "QU1": _b(144, CODE), "QU1S": _b(144, U8), "QV": _b(128, CODE), "QVS": _b(128, U8),
     "WC": _b(512, CODE), "WS": _b(512, U8), "QX": _b(512, CODE), "QXS": _b(512, U8),
-    "PI": _b(28, I32), "PIX": _b(1, I32), "PMI": _b(1, I32), "GI": _b(1, I32),
-    "DUP0": _b(2, U16), "DUP1": _b(2, U16), "U1L": _b(8, U16),
-    "PM": _b(1), "PF": _b(1), "NG": _b(1), "NG16": _b(1), "GQ": _b(1), "WQ": _b(1), "PD": _b(456), "IO4": _b(1792), "MD": _b(448), "MASK": _b(448),
-    "A16": _b(28), "Z8": _b(8), "NS": _b(4), "RUN": _b(32), "LJ": _b(32), "LV": _b(4), "CF": _b(4),
-    "NAT": _b(32), "TT": _b(32), "LT0": _b(32), "LT1": _b(32), "LR": _b(64), "RM": _b(448), "SC": _b(232), "SCa": _b(120), "SCb": _b(120), "YS": _b(448),
+    "PI": _b(28, I32), "PIX": _b(1, I32), "PMI": _b(1, I32), "GI": _b(1, I32), "PQI": _b(1, I32), "PEI": _b(1, I32),
+    "DUP0": _b(2, U16), "DUP1": _b(2, U16), "U1L": _b(10, U16), "OF": _b(112, U16), "EL": _b(112, U16),
+    "TB": _b(7 * C, BF), "PD": _b(448, BF), "VR": _b(448, BF), "SC": _b(448, "float16"), "MASK": _b(448, BF),
+    "MD": _b(448), "HS": _b(1792), "YS": _b(448), "YO": _b(448),
+    "Z2": _b(2), "NB": _b(40), "RS": _b(40), "RUN": _b(40), "LJ": _b(32), "LV": _b(4), "CF": _b(4),
 }
-for _i in ("EL", "RK", "RK1", "OL", "OF0", "OF1", "OF2", "OF3"):
+for _i in ("PM", "PF", "NG", "PQ", "PE", "PO", "u1", "u2", "u3"):
+    SCRATCH[_i] = _b(1)
+for _i in ("RK", "RK1", "OL", "PL"):
     SCRATCH[_i] = _b(28, U16)
-for _i in ("JW", "PW", "JP", "JD", "PDF", "KK", "Q", "wf", "lm", "mq", "a1", "a2", "al", "b1", "b2", "m1", "m2", "m3", "k1", "k2", "k3", "dc", "ED", "D1", "D2", "D3"):
+for _i in ("A16", "JW", "y1", "y2", "y3", "r1", "wf", "lm", "o1", "o2"):
     SCRATCH[_i] = _b(28)
 for _i in range(4):
-    SCRATCH["X%d" % _i] = _b(1792, BF)
-    SCRATCH["HS%d" % _i] = _b(448)
-    SCRATCH["DR%d" % _i] = _b(448)
+    SCRATCH["X%d" % _i] = _b(2048, BF)
 for _i in range(R):
     for _n in ("QZ", "LZ"):
         SCRATCH["%s%d" % (_n, _i)] = _b(448, CODE)
@@ -39,7 +45,7 @@ for _i in range(R):
 
 SEMAPHORES = ["sv", "ss", "st", "sg", "loc"]
 SEMAPHORES += ["ld%d" % _i for _i in range(8)] + ["sto%d" % _i for _i in range(12)]
-SEMAPHORES += ["ar%d%d%s" % (_t, _h, _k) for _t in range(R) for _h in range(2) for _k in "cs"]
+SEMAPHORES += ["ar%d%d" % (_t, _h) for _t in range(R) for _h in range(len(ZP))]
 
 
 def rank_program(g, core, T, topo):
@@ -110,6 +116,12 @@ def rank_program(g, core, T, topo):
     def act(out, a, f, reads, writes, **kw):
         do("s", S.activation, (out, a, f), reads, writes, **kw)
 
+    def move(qn, out, a, reads, writes):
+        if qn == "v":
+            vcopy(out, a, reads, writes)
+        else:
+            act(out, a, F.Copy, reads, writes)
+
     def scan(out, a, b, init, o0, o1, reads, writes):
         do("v", V.tensor_tensor_scan, (out, a, b, init, o0, o1), reads, writes)
 
@@ -122,293 +134,318 @@ def rank_program(g, core, T, topo):
     def fill(ap, c, key):
         do("v", V.memset, (ap, c), [], [key])
 
-    def iota(out, pattern, key, mult=0, flag=True):
+    def iota(out, pattern, key, mult=0, flag=True, base=0):
         kw = {"allow_small_or_imprecise_dtypes": True} if flag else {}
-        do("g", g.iota, (out, pattern, 0, mult), [], [key], **kw)
+        do("g", g.iota, (out, pattern, base, mult), [], [key], **kw)
 
-    dma("y", "ld0", T.X0[:, 0:1024], T.x[:, 0:1024], [], ["X0h0"])
-    dma("s", "ld1", T.UT[:, :], T.u[:, :], [], ["UT"])
-    dma("s", "ld2", T.PI[:, :], T.p[:, :], [], ["PI"])
-    dma("y", "ld3", T.X0[:, 1024:1792], T.x[:, 1024:1792], [], ["X0h1"])
-    dma("y", "ld4", T.WC[:, :].bitcast(dt.uint8), T.wc[:, :], [], ["WC"])
-    dma("y", "ld5", T.WS[:, :], T.ws[:, :], [], ["WS"])
-    dma("y", "ld6", T.VT[:, :], T.v[:, :], [], ["VT"])
+    def runs(name, a, b, n=32):
+        return ["%s.%d" % (name, i) for i in range(a // n, (b - 1) // n + 1)]
+
+    def row(t, a=0, b=C):
+        return T.TB[:, (R - t) * C + a:(R - t) * C + b]
+
+    dma("s", "ld0", T.UT[:, :], T.u[:, :], [], ["UT"])
+    for i, (a, b) in enumerate(XL):
+        dma("y", "ld%d" % (1 + i), T.X0[:, 4 * a:4 * b], T.x[:, 4 * a:4 * b], [], runs("X0", a, b))
+    dma("s", "ld4", T.PI[:, :], T.p[:, :], [], ["PI"])
+    dma("y", "ld5", T.WC[:, :].bitcast(dt.uint8), T.wc[:, :], [], ["WC"])
+    dma("y", "ld6", T.WS[:, :], T.ws[:, :], [], ["WS"])
+    dma("y", "ld7", T.VT[:, :], T.v[:, :], [], ["VT"])
 
     iota(T.PIX[:, :], [[0, 1]], "PIX", 1, False)
+    iota(T.MD[:, :], [[0, 112], [1, 4]], "MD")
+    iota(T.TB[:, TI:TI + C], [[1, C]], "IO", base=-MID)
     iota(T.A16[:, :], [[16, 28]], "A16")
-    iota(T.MD[:, :], [[0, 28], [1, 16]], "MD")
-    iota(T.IO4[:, :], [[1, 448], [0, 4]], "IO4")
+    for t in range(1, R + 1):
+        iota(T["X%d" % t][:, 4 * C:2048], [[0, 256]], "X%dz" % t)
     fill(T.U1L[:, :], 1, "U1L")
-    fill(T.ZT[:, :], 0.0, "ZT")
-    fill(T.Z8[:, :], 0.0, "Z8")
-    fill(T.SC[:, :], 0.0, "SC")
-    fill(T.SCa[:, :], 0.0, "SCa")
-    fill(T.SCb[:, :], 0.0, "SCb")
-    fill(T.PD[:, NIL:456], 0.0, "PDz")
-    fill(T.TT[:, :], 0.0, "TT")
-    quant(T.QX[:, 384:512], T.QXS[:, 384:512], T.ZT[:, :], ["ZT"], ["QXh1", "QXz"])
+    fill(T.X0[:, 4 * C:2048], 0.0, "X0z")
+    fill(T.Z2[:, :], 0.0, "Z2")
     ts(T.PMI[:, :], T.PIX[:, :], 15, None, [A.bitwise_and], ["PIX"], ["PMI"])
     ts(T.GI[:, :], T.PIX[:, :], 4, None, [A.arith_shift_right], ["PIX"], ["GI"])
-    vcopy(T.PF[:, :], T.PIX[:, :], ["PIX"], ["PF"])
     vcopy(T.PM[:, :], T.PMI[:, :], ["PMI"], ["PM"])
-    ts(T.NG[:, :], T.GI[:, :], -1.0, -225.0, [A.mult, A.add], ["GI"], ["NG"])
-    ts(T.NG16[:, :], T.GI[:, :], -1.0, -241.0, [A.mult, A.add], ["GI"], ["NG16"])
-    ts(T.GQ[:, :], T.GI[:, :], 448.0, 448.0 * 242, [A.mult, A.add], ["GI"], ["GQ"])
-    fill(T.WQ[:, :], -448.0 * 447, "WQ")
-    for e in range(2):
-        ts(T["DUP%d" % e][:, :], T.Z8[:, 0:2], T.PM[:, 0:1], 16.0 * e, [A.add, A.add], ["Z8", "PM"], ["DUP%d" % e])
-    ts(T.JW[:, :], T.A16[:, :], T.PM[:, 0:1], None, [A.add], ["A16", "PM"], ["JW"])
+    ts(T.u1[:, :], T.PMI[:, :], 16.0, -1.0, [A.mult, A.add], ["PMI"], ["u1"])
+    ts(T.PF[:, :], T.PIX[:, :], -float(MID), None, [A.add], ["PIX"], ["PF"])
+    ts(T.u2[:, :], T.PM[:, :], 8.0, T.u1[:, 0:1], [A.is_lt, A.mult], ["PM", "u1"], ["u2"])
+    ts(T.PQI[:, :], T.PMI[:, :], 2, None, [A.arith_shift_right], ["PMI"], ["PQI"])
+    ts(T.u3[:, :], T.PM[:, :], 8.0, T.u2[:, 0:1], [A.is_equal, A.add], ["PM", "u2"], ["u3"])
+    ts(T.PEI[:, :], T.PIX[:, :], 3, None, [A.bitwise_and], ["PIX"], ["PEI"])
+    ts(T.U1L[:, 0:1], T.u3[:, :], 1.0, None, [A.add], ["u3", "U1L"], ["U1L"])
+    vcopy(T.PQ[:, :], T.PQI[:, :], ["PQI"], ["PQ"])
+    vcopy(T.PE[:, :], T.PEI[:, :], ["PEI"], ["PE"])
+    fill(T.RS[:, :], 0.0, "RS")
+    ts(T.NG[:, :], T.GI[:, :], -1.0, None, [A.mult], ["GI"], ["NG"])
+    fill(T.RS[:, 0:40:10], BIG, "RS")
+    ts(T.u1[:, :], T.PQ[:, :], 2048.0, 4.0 * MID - 3 * 2048, [A.mult, A.add], ["PQ"], ["u1"])
+    fill(T.TT[:, :], 0.0, "TT")
+    tt(T.PO[:, :], T.u1[:, :], T.PE[:, :], A.add, ["u1", "PE"], ["PO"])
+    ts(T.YO[:, :], T.MD[:, :], T.PQ[:, 0:1], 8704.0, [A.is_gt, A.mult], ["MD", "PQ"], ["YO"])
+    act(T.MASK[:, :], T.YO[:, :], F.Identity, ["YO"], ["MASK"], bias=-8192.0)
 
-    quant(T.QU[:, :], T.QUS[:, :], T.UT[:, :], ["UT"], ["QU"])
-    vcopy(T.QU1[:, :].bitcast(dt.uint32), T.QU[:, 0:128].bitcast(dt.uint32).indirect(T.U1L[:, 0:8]), ["QU", "U1L"], ["QU1c"])
-    act(T.QU1S[:, :], T.QUS[:, 0:128].indirect(T.U1L[:, 0:8]), F.Copy, ["QU", "U1L"], ["QU1s"])
+    def late_constants():
+        ts(T.THR[:, :], T.TB[:, TI:TI + 128], T.PF[:, 0:1], 0.5, [A.is_gt, A.subtract], ["IO", "PF"], ["THR"])
+        for e in range(2):
+            ts(T["DUP%d" % e][:, :], T.Z2[:, 0:2], T.PM[:, 0:1], 16.0 * e, [A.add, A.add], ["Z2", "PM"], ["DUP%d" % e])
+        ts(T.JW[:, :], T.A16[:, :], T.PM[:, 0:1], None, [A.add], ["A16", "PM"], ["JW"])
 
-    def quant_x(t, h):
-        a, b = H[h]
-        quant(T.QX[:, a:b], T.QXS[:, a:b], T["X%d" % t][:, 4 * a:4 * b], ["X%dh%d" % (t, h)], ["QXh%d" % h])
+    def quant_x(t, m):
+        a = 128 * m
+        quant(T.QX[:, a:a + 128], T.QXS[:, a:a + 128], T["X%d" % t][:, 4 * a:4 * a + 512],
+              runs("X%d" % t, a, min(a + 128, C)) + (["X%dz" % t] if m == 3 else []), ["QX%d" % m])
 
-    def products(h):
-        a, b = H[h]
-        for m in (0, 1) if h == 0 else (2, 3):
-            mm(m, 128, T.QX[:, 128 * m:128 * m + 128], T.QXS[:, 128 * m:128 * m + 128], T.QU[:, :], T.QUS[:, :],
-               ["QXh%d" % h, "QU"] + (["QXz"] if m == 3 else []))
-        mm(4 + h, b - a, T.QU1[:, :], T.QU1S[:, :], T.QX[:, a:b], T.QXS[:, a:b], ["QXh%d" % h, "QU1c", "QU1s"])
+    UK = ["QU1c", "QU1s"]
+    ROWS = [4, 5, 6, 7]
+
+    def products(m):
+        a = 128 * m
+        mm(m % 2, 128, T.QX[:, a:a + 128], T.QXS[:, a:a + 128], T.QU1[:, 0:128], T.QU1S[:, 0:128], ["QX%d" % m] + UK)
+        lo = a if m == 3 else 0
+        for bank in [ROWS[m]] + ([2] if m == 3 else []):
+            mm(bank, a + 128 - lo, T.QU1[:, 16:144], T.QU1S[:, 16:144], T.QX[:, lo:a + 128], T.QXS[:, lo:a + 128],
+               ["QX%d" % k for k in range(lo // 128, m + 1)] + UK)
 
     def negs(m):
-        act(T.NS[:, m:m + 1], T.PS[:, 512 * m + 1:512 * m + 2], F.Copy, ["bk%d" % m], ["NS%d" % m], scale=-1.0)
+        act(T.NB[:, 10 * m:10 * m + 10], T.PS[:, 512 * (m % 2):512 * (m % 2) + 10], F.Copy, ["bk%d" % (m % 2)], ["NB%d" % m], scale=-1.0)
 
-    def sign(m, h):
-        a, b = H[h]
-        act(T.SG[:, 448 * m + a:448 * m + b], T.PS[:, 512 * (4 + h):512 * (4 + h) + b - a], F.Sign,
-            ["bk%d" % (4 + h), "NS%d" % m], ["SG%d%d" % (m, h)], bias=T.NS[:, m:m + 1])
+    def sign(m, a, b, k):
+        o = 512 * ROWS[k] - (384 if k == 3 else 0)
+        act(T.SG[:, C * m + a:C * m + b], T.PS[:, o + a:o + b], F.Sign, ["bk%d" % ROWS[k], "NB%d" % m], runs("SG%d" % m, a, b, 128),
+            bias=T.NB[:, 10 * m + 9:10 * m + 10])
 
-    def runmax(m):
-        scan(T.RUN[:, 8 * m:8 * m + 8], T.Z8[:, :], T.PS[:, 512 * m:512 * m + 128:16], BIG, A.add, A.max, ["Z8", "bk%d" % m, "NS%d" % m], ["RUN%d" % m])
+    def signs(k):
+        negs(k)
+        if k == 3:
+            sign(3, 0, 384, 2)
+            sign(3, 384, C, 3)
+            return
+        if k == 2:
+            level(0); level(1)
+        sign(k, 0, 128 * k + 128, k)
+        for m in range(k):
+            sign(m, 128 * k, 128 * k + 128, k)
+
+    def runmin(a, b):
+        scan(T.RUN[:, 10 * a:10 * b], T.RS[:, 10 * a:10 * b], T.NB[:, 10 * a:10 * b], 0.0, A.add, A.min,
+             ["RS"] + ["NB%d" % m for m in range(a, b)], ["RUN%d" % m for m in range(a, b)])
 
     def level(m):
-        act(T.LJ[:, 8 * m:8 * m + 8], T.RUN[:, 8 * m:8 * m + 8], F.Sign, ["RUN%d" % m], ["LJ%d" % m, "LV%d" % m],
-            bias=T.RUN[:, 8 * m + 7:8 * m + 8], scale=-1.0, accum_out=T.LV[:, m:m + 1])
+        act(T.LJ[:, 8 * m:8 * m + 8], T.RUN[:, 10 * m:10 * m + 8], F.Sign, ["RUN%d" % m], ["LJ%d" % m, "LV%d" % m],
+            bias=T.RUN[:, 10 * m + 7:10 * m + 8], scale=-1.0, accum_out=T.LV[:, m:m + 1])
 
-    def before(m, a, b, kind):
-        o = 448 * m
-        rd = ["SG%d%d" % (m, h) for h in (0, 1) if a < H[h][1] and b > H[h][0]]
-        if kind == "tri":
-            tt(T.CM[:, o + a:o + b], T.SG[:, o + a:o + b], T.THR[:, 0:b - a], A.is_gt, rd + ["THR"], ["CM%d.%d" % (m, a)])
+    def before(m, a, b):
+        o = C * m
+        rd, wr = runs("SG%d" % m, a, b, 128), runs("CM%d" % m, a, b, 128)
+        if a == 128 * m:
+            tt(T.CM[:, o + a:o + b], T.SG[:, o + a:o + b], T.THR[:, 0:b - a], A.is_gt, rd + ["THR"], wr)
         else:
-            ts(T.CM[:, o + a:o + b], T.SG[:, o + a:o + b], 0.0, None, [kind], rd, ["CM%d.%d" % (m, a)])
+            ts(T.CM[:, o + a:o + b], T.SG[:, o + a:o + b], 0.0, None, [A.is_ge if a < 128 * m else A.is_gt], rd, wr)
 
-    def count(m, parts):
-        o = 448 * m
-        scan(T.SCN[:, 224 * m:224 * m + 224], T.CM[:, o:o + 224], T.CM[:, o + 224:o + 448], -225.0, A.add, A.add,
-             ["CM%d.%d" % (m, a) for a in parts], ["SCN%d" % m])
+    def last_run(m):
+        ts(T.CM[:, C * m + 384:C * m + C], T.PS[:, 1024:1088], T.NB[:, 10 * m + 9:10 * m + 10], 0.0, [A.add, A.is_gt],
+           ["bk2", "NB%d" % m], ["CM%d.3" % m])
 
-    def vv(o, a, b, op):
-        tt(T[o][:, 0:28], T[a][:, 0:28], T[b][:, 0:28], op, (LRK if a == "LR" else [a]) + [b], [o])
-
-    def prep(t, o):
-        vv(o, {"JD": "JW", "PDF": "PW", "KK": "JP"}[o], "D%d" % t if t else "PW", A.subtract)
-
-    def scores_head():
-        negs(0); negs(1)
-        sign(0, 0); sign(1, 0)
+    def count(m):
+        o = C * m
+        scan(T.SCN[:, 224 * m:224 * m + 224], T.CM[:, o:o + 224], T.CM[:, o + 224:o + C], -225.0, A.add, A.add,
+             runs("CM%d" % m, 0, C, 128), ["SCN%d" % m])
 
     def scores_tail():
-        level(0); level(1)
-        negs(2); negs(3)
-        sign(2, 0); sign(3, 0)
-        for m in range(4):
-            sign(m, 1)
-        before(1, 0, 128, A.is_ge)
-        before(0, 0, 128, "tri")
-        before(1, 128, 256, "tri")
-        runmax(2); runmax(3)
+        before(2, 0, 256)
+        last_run(0); last_run(1); last_run(2)
+        before(2, 256, 384)
+        runmin(2, 4)
         level(2); level(3)
-        ts(T.CF[:, :], T.PS[:, 2:2048:512], 0.0, 16.0, [A.is_gt, A.mult], ["bk0", "bk1", "bk2", "bk3"], ["CF"])
-        before(2, 0, 256, A.is_ge)
-        before(3, 0, 256, A.is_ge)
-        before(0, 128, 448, A.is_gt)
-        before(1, 256, 448, A.is_gt)
-        count(0, [0, 128])
-        before(2, 256, 384, "tri")
-        count(1, [0, 128, 256])
-        before(2, 384, 448, A.is_gt)
-        before(3, 384, 448, "tri")
-        before(3, 256, 384, A.is_ge)
-        count(2, [0, 256, 384])
-        count(3, [0, 256, 384])
-        tt(T.SCN[:, 4 * 224 + 223:1792:224], T.LV[:, :], T.CF[:, :], A.add, ["LV0", "LV1", "LV2", "LV3", "CF"], ["SCNw"])
+        before(0, 128, 384)
+        before(1, 256, 384)
+        count(2)
+        ts(T.CF[:, :], T.NB[:, 8:40:10], 0.0, 16.0, [A.is_lt, A.mult], ["NB0", "NB1", "NB2", "NB3"], ["CF"])
+        count(0)
+        before(3, 0, 384)
+        before(3, 384, C)
+        count(1)
+        count(3)
+        tt(T.SCN[:, 4 * 224 + 223:1792:224], T.CF[:, :], T.LV[:, :], A.subtract, ["LV0", "LV1", "LV2", "LV3", "CF"], ["SCNw"])
 
     LRK = ["LRe0", "LRe1", "LR1", "LR2", "LR3"]
     RKK = ["RK%d" % b for b in range(4)]
 
-    def lists(t):
+    def lists():
         rd = ["SCN0", "SCN1", "SCN2", "SCN3", "SCNw"]
-        prep(t, "JD")
-        for b in range(4):
-            ts(T.NAT[0:32, b:32:4], T.SCN[32 * b:32 * b + 32, 223:1792:224], 225.0, None, [A.add], rd, ["NAT%d" % b])
-        prep(t, "PDF")
-        do("v", V.transpose, (T.TT[0:32, 0:32], T.NAT[0:32, 0:32]), ["NAT%d" % b for b in range(4)], ["TT"])
-        prep(t, "KK")
+        for b in range(1, 4):
+            vcopy(T.SCN[0:32, 223 + 56 * b:1968:224], T.SCN[32 * b:32 * b + 32, 223:1792:224], rd, ["NAT%d" % b])
+        do("v", V.transpose, (T.TT[0:32, 0:32], T.SCN[0:32, 223:1968:56]), rd + ["NAT1", "NAT2", "NAT3"], ["TT"])
         for e in range(2):
             vcopy(T["LT%d" % e][:, :], T.TT[:, 0:32].indirect(T["DUP%d" % e][:, 0:2]), ["TT", "DUP%d" % e], ["LT%d" % e])
         for e in range(2):
             do("v", V.transpose, (T.LR[0:32, e:64:2], T["LT%d" % e][0:32, 0:32]), ["LT%d" % e], ["LRe%d" % e])
         for b in range(4):
-            ts(T.RK[32 * b:32 * b + 32, :], T.LR[0:32, 0:28], -1.0, None, [A.add], ["LRe0", "LRe1"], ["RK%d" % b])
+            ts(T.RK[32 * b:32 * b + 32, :], T.LR[0:32, 0:28], 224.0, None, [A.add], ["LRe0", "LRe1"], ["RK%d" % b])
         for b in range(1, 4):
             act(T.LR[32 * b:32 * b + 32, 0:64], T.LR[0:32, 0:64], F.Copy, ["LRe0", "LRe1"], ["LR%d" % b])
 
-    def sorted_row(t):
-        vcopy(T.PD[:, 0:448].indirect(T.RK[:, 0:28]), T["DR%d" % t][:, :], RKK + ["DR%d" % t], ["PD"])
+    def sort(win, t, a, b, key):
+        vcopy(win.indirect(T.RK[:, a // 16:b // 16]), row(t, a, b), RKK + runs("DR%d" % t, a, b), [key])
+
+    def fold(src, keys, a, b):
+        scan(T.SC[:, a:b], T.MASK[:, a:b], src, 0.0, A.add, A.max, ["MASK"] + keys, runs("SC", a, b))
+
+    def four(name, a, b):
+        ts(T[name][:, a // 4:b // 4], T.SC[:, a + 3:b:4], 4.0, T.PO[:, 0:1], [A.mult, A.add], runs("SC", a, b) + ["PO"], runs(name, a, b))
 
     def pointers(t):
-        k = "D%d" % t if t else "PW"
-        W = T.LR[:, 32:60]
-        sorted_row(t)
-        act(T.wf[:, :], T.LR[:, 0:28], F.Relu, LRK + ["WQ"], ["wf"], bias=T.WQ[:, 0:1], scale=448.0)
-        act(T.Q[:, :], W, F.Relu, LRK + ["GQ"], ["Q"], bias=T.GQ[:, 0:1], scale=-448.0)
-        act(T.a1[:, :], W, F.Sign, LRK + ["NG16"], ["a1"], bias=T.NG16[:, 0:1])
-        act(T.a2[:, :], W, F.Sign, LRK + ["NG"], ["a2"], bias=T.NG[:, 0:1])
-        act(T.b1[:, :], T.a1[:, :], F.Square, ["a1"], ["b1"])
-        act(T.b2[:, :], T.a2[:, :], F.Square, ["a2"], ["b2"])
-        act(T.al[:, :], T.a1[:, :], F.Relu, ["a1"], ["al"])
-        vv("lm", "LR", "wf", A.subtract)
-        vv("m1", "b1", "JD", A.mult)
-        vv("mq", "lm", "Q", A.max)
-        vv("m2", "b2", "PDF", A.mult)
-        ts(T.OL[:, :], T.mq[:, :], float(NIL), None, [A.min], ["mq"], ["OL"])
-        vv("m3", "al", k, A.mult)
-        tt(T.RM[:, :], T.PD[:, 0:456].indirect(T.OL[:, 0:28]), T.MASK[:, :], A.mult, ["PD", "PDz", "OL", "MASK"], ["RM"])
-        vv("k1", "KK", "m1", A.subtract)
-        scan(T.SC[:, 1:225], T.RM[:, 0:448:2], T.RM[:, 1:448:2], 0.0, A.add, A.add, ["RM"], ["SC"])
-        vv("k2", "m2", "m3", A.add)
-        tt(T.dc[:, :], T.SC[:, 8:225:8], T.SC[:, 0:217:8], A.subtract, ["SC"], ["dc"])
-        vv("k3", "k1", "k2", A.subtract)
-        vcopy(T.RK1[:, :], T.lm[:, :], ["lm"], ["RK1"])
-        n = "D%d" % (t + 1)
-        vv(n, "dc", "k3", A.add)
-        for e in (2, 0, 3, 1):
-            ts(T["OF%d" % e][:, :], T[n][:, :], 4.0, float(e), [A.mult, A.add], [n], ["OF%d" % e])
+        d, s = C * (t + 1), C * (t + 2)
+        act(T.y1[:, :], T.LR[:, 32:60], F.Abs, LRK + ["NG"], ["y1"], bias=T.NG[:, 0:1])
+        act(T.r1[:, :], T.LR[:, 0:28], F.Identity, LRK, ["r1"], bias=225.0 + s + C)
+        act(T.y2[:, :], T.y1[:, :], F.Abs, ["y1"], ["y2"], bias=-(d + 15 * s) / 2, scale=float(s))
+        act(T.wf[:, :], T.LR[:, 0:28], F.Relu, LRK, ["wf"], bias=-222.0 * C, scale=float(C))
+        act(T.y3[:, :], T.y2[:, :], F.Relu, ["y2"], ["y3"], bias=-(15 * s - d) / 2)
+        sort(T.TB[:, TS:TS + C], t, 0, 288, "TBs")
+        tt(T.o1[:, :], T.y3[:, :], T.JW[:, :], A.add, ["y3", "JW"], ["o1"])
+        tt(T.lm[:, :], T.r1[:, :], T.wf[:, :], A.subtract, ["r1", "wf"], ["lm"])
+        sort(T.TB[:, TS:TS + C], t, 288, 384, "TBs")
+        tt(T.o2[:, :], T.o1[:, :], T.lm[:, :], A.min, ["o1", "lm"], ["o2"])
+        sort(T.TB[:, TS:TS + C], t, 384, C, "TBs")
+        vcopy(T.OL[:, :], T.o2[:, :], ["o2"], ["OL"])
+        ts(T.RK1[:, :], T.lm[:, :], -float(s + C), None, [A.add], ["lm"], ["RK1"])
+
+    def pick(qn, t, a, b):
+        rd = ["TBs", "OL", "IO", "P0"] + [k for i in range(t + 1) for k in runs("DR%d" % i, 0, C)]
+        move(qn, row(t + 1, a, b), T.TB[:, (R - t) * C:7 * C].indirect(T.OL[:, a // 16:b // 16]), rd, runs("DR%d" % (t + 1), a, b))
 
     def send(t, h):
-        a, b = HZ[h]
+        a, b = ZP[h]
         dst = T.cores[(rank + 1 + t) % N]
         rid, pid, _ = topo.addr(dst)
         m = topo.mask(core, dst)
         waits("g", ["QZ%dh%d" % (t, h)], [])
         g.remote_dma(T["LZ%d" % t][:, a:b].bitcast(dt.uint8), T["QZ%d" % t][:, a:b].bitcast(dt.uint8),
-                     T.sem["ar%d%dc" % (t, h)], T.sem.loc, pid, rid, m)
-        g.remote_dma(T["LZS%d" % t][:, a:b], T["QZS%d" % t][:, a:b], T.sem["ar%d%ds" % (t, h)], T.sem.loc, pid, rid, m)
+                     T.sem["ar%d%d" % (t, h)], T.sem.loc, pid, rid, m)
+        g.remote_dma(T["LZS%d" % t][:, a:b], T["QZS%d" % t][:, a:b], T.sem["ar%d%d" % (t, h)], T.sem.loc, pid, rid, m)
         cnt["loc"] = cnt.get("loc", 0) + 2 * len(topo.engines(core, dst))
-        e = len(topo.engines(T.cores[(rank - 1 - t) % N], core))
-        lastw["LZ%dh%d" % (t, h)] = ("ar%d%dc" % (t, h), e, None)
-        lastw["LZS%dh%d" % (t, h)] = ("ar%d%ds" % (t, h), e, None)
+        lastw["LZ%dh%d" % (t, h)] = ("ar%d%d" % (t, h), 2 * len(topo.engines(T.cores[(rank - 1 - t) % N], core)), None)
 
     def mosaic(t):
-        X = T["X%d" % t]
-
-        def part(h, e):
-            a, b = HZ[h]
-            o, i = T.Z[:, 4 * a + e:4 * b:4], X[:, 0:1792].indirect(T["OF%d" % e][:, a // 16:b // 16])
-            rd, wr = ["X%dh0" % t, "X%dh1" % t, "OF%d" % e], ["Zh%d.%d" % (h, e)]
-            if e >= 2:
-                act(o, i, F.Copy, rd, wr)
-            else:
-                vcopy(o, i, rd, wr)
+        def part(qn, a, b):
+            move(qn, T.Z[:, 4 * a:4 * b], T["X%d" % t][:, 0:4 * C].indirect(T.OF[:, a // 4:b // 4]),
+                 runs("X%d" % t, 0, C) + runs("OF", a, b), runs("Z", a, b, 8))
 
         def pack(h):
-            a, b = HZ[h]
-            quant(T["QZ%d" % t][:, a:b], T["QZS%d" % t][:, a:b], T.Z[:, 4 * a:4 * b],
-                  ["Zh%d.%d" % (h, e) for e in range(4)], ["QZ%dh%d" % (t, h)])
+            a, b = ZP[h]
+            quant(T["QZ%d" % t][:, a:b], T["QZS%d" % t][:, a:b], T.Z[:, 4 * a:4 * b], runs("Z", a, b, 8), ["QZ%dh%d" % (t, h)])
             send(t, h)
 
-        for h in range(2):
-            part(h, 2); part(h, 3)
-        for h in range(2):
-            part(h, 0); part(h, 1)
-            pack(h)
-        act(T["DR%d" % (t + 1)][:, :], T.IO4[:, :].indirect(T.OF0[:, 0:28]), F.Copy, ["IO4", "OF0"], ["DR%d" % (t + 1)])
+        for c in MOSAIC:
+            if c[0] == "pick":
+                pick(c[1], t, c[2], c[3])
+            elif c[0] == "fold":
+                fold(row(t + 1, c[1], c[2]), runs("DR%d" % (t + 1), c[1], c[2]), c[1], c[2])
+            elif c[0] == "four":
+                four("OF", c[1], c[2])
+            elif c[0] == "part":
+                part(*c[1:])
+            else:
+                pack(c[1])
 
     def join_list(t):
-        sorted_row(t + 1)
-        for h, s in enumerate("ab"):
-            tt(T.RM[:, 224 * h:224 * h + 224], T.PD[:, 0:456].indirect(T.RK1[:, 14 * h:14 * h + 14]), T.MASK[:, 224 * h:224 * h + 224], A.mult,
-               ["PD", "PDz", "RK1", "MASK", "RM"], ["RM" + s])
-        for h, s in enumerate("ab"):
-            o = 224 * h
-            scan(T["SC" + s][:, 1:113], T.RM[:, o:o + 224:2], T.RM[:, o + 1:o + 224:2], 0.0, A.add, A.add, ["RM" + s], ["SC" + s])
-        for h, s in enumerate("ab"):
-            tt(T.ED[:, 14 * h:14 * h + 14], T["SC" + s][:, 8:113:8], T["SC" + s][:, 0:105:8], A.subtract, ["SC" + s], ["ED" + s])
-        for h, s in enumerate("ab"):
-            vcopy(T.EL[:, 14 * h:14 * h + 14], T.ED[:, 14 * h:14 * h + 14], ["ED" + s], ["EL" + s])
-
-    def layer(t):
+        sort(T.PD[:, 0:C], t + 1, 0, C, "PD")
+        for h, qn in enumerate("vv"):
+            a, b = 224 * h, 224 * h + 224
+            move(qn, T.VR[:, a:b], T.PD[:, 0:C].indirect(T.RK1[:, a // 16:b // 16]), ["PD", "RK1"], runs("VR", a, b))
         for h in range(2):
-            a, b = HZ[h]
-            for w in range(4):
-                mm(2 * w + h, b - a, T.WC[:, 128 * w:128 * w + 128], T.WS[:, 128 * w:128 * w + 128], T["LZ%d" % t][:, a:b], T["LZS%d" % t][:, a:b],
-                   ["WC", "WS", "LZ%dh%d" % (t, h), "LZS%dh%d" % (t, h)])
-        for w, h in ((0, 0), (1, 0), (0, 1), (2, 0), (1, 1), (3, 0), (2, 1), (3, 1)):
-            a, b = HZ[h]
-            bk = 2 * w + h
-            act(T["HS%d" % w][:, a:b], T.PS[:, 512 * bk:512 * bk + b - a], F.Copy, ["bk%d" % bk], ["HS%dh%d" % (w, h)], scale=0.00390625)
+            a, b = 224 * h, 224 * h + 224
+            fold(T.VR[:, a:b], runs("VR", a, b), a, b)
+        for h in range(2):
+            four("EL", 224 * h, 224 * h + 224)
 
-    def join(t, h, ws=range(4)):
-        a, b = H[h]
-        for w in ws:
-            tt(T["X%d" % (t + 1)][:, 4 * a + w:4 * b:4], T["HS%d" % w][:, 0:448].indirect(T.EL[:, a // 16:b // 16]),
-               T["X%d" % t][:, 4 * a + w:4 * b:4], A.add, ["HS%dh0" % w, "HS%dh1" % w, "ELa", "ELb", "X%dh%d" % (t, h)], ["X%dh%d.%d" % (t + 1, h, w)])
-        lastw["X%dh%d" % (t + 1, h)] = lastw["X%dh%d.%d" % (t + 1, h, ws[-1])]
+    def layer(t, h):
+        a, b = ZP[h]
+        last = h == len(ZP) - 1
+        for w in range(4):
+            mm(4 * (h % 2) + w, b - a, T.WC[:, 128 * w:128 * w + 128], T.WS[:, 128 * w:128 * w + 128], T["LZ%d" % t][:, a:b], T["LZS%d" % t][:, a:b],
+               ["WC", "WS", "LZ%dh%d" % (t, h)])
+        for w in range(4):
+            bk = 4 * (h % 2) + w
+            o, i, rd, wr = T.HS[:, 4 * a + w:4 * b:4], T.PS[:, 512 * bk:512 * bk + b - a], ["bk%d" % bk], ["HS%dh%d" % (w, h)]
+            if last and w % 2:
+                ts(o, i, 0.00390625, None, [A.mult], rd, wr)
+            else:
+                act(o, i, F.Copy, rd, wr, scale=0.00390625)
 
-    quant_x(0, 0)
-    products(0)
-    scores_head()
-    quant_x(0, 1)
-    products(1)
-    vcopy(T.PW[:, :], T.PI[:, :], ["PI"], ["PW"])
-    ts(T.OF0[:, :], T.PI[:, :], 4.0, None, [A.mult], ["PI"], ["OF0"])
-    runmax(0); runmax(1)
-    ts(T.MASK[:, :], T.MD[:, :], T.PM[:, 0:1], None, [A.is_equal], ["MD", "PM"], ["MASK"])
-    vv("JP", "JW", "PW", A.add)
-    ts(T.THR[:, :], T.IO4[:, 0:512:4], T.PF[:, 0:1], 0.5, [A.is_gt, A.subtract], ["IO4", "PF"], ["THR"])
+    HK = ["HS%dh%d" % (w, h) for w in range(4) for h in range(len(ZP))]
+
+    def join(t, a, b):
+        tt(T["X%d" % (t + 1)][:, 4 * a:4 * b], T.HS[:, 0:4 * C].indirect(T.EL[:, a // 4:b // 4]), T["X%d" % t][:, 4 * a:4 * b], A.add,
+           HK + runs("EL", a, b) + runs("X%d" % t, a, b), runs("X%d" % (t + 1), a, b))
+
+    def score(t, m):
+        quant_x(t, m)
+        products(m)
+        signs(m)
+
+    quant(T.QU[:, :], T.QUS[:, :], T.UT[:, :], ["UT"], ["QU"])
+    vcopy(T.QU1[:, :].bitcast(dt.uint32), T.QU[:, 0:128].bitcast(dt.uint32).indirect(T.U1L[:, 0:9]), ["QU", "U1L"], ["QU1c"])
+    act(T.QU1S[:, :], T.QUS[:, 0:128].indirect(T.U1L[:, 0:9]), F.Copy, ["QU", "U1L"], ["QU1s"])
+    score(0, 0)
+    late_constants()
+    score(0, 1)
+    vcopy(T.PL[:, :], T.PI[:, :], ["PI"], ["PL"])
+    before(0, 0, 128)
+    runmin(0, 2)
+    score(0, 2)
+    score(0, 3)
+    before(1, 0, 128)
+    before(1, 128, 256)
     scores_tail()
-    act(T.DR0[:, :], T.IO4[:, :].indirect(T.OF0[:, 0:28]), F.Copy, ["IO4", "OF0"], ["DR0"])
+    act(row(0), T.TB[:, TI:TI + C].indirect(T.PL[:, 0:28]), F.Copy, ["IO", "PL"], runs("DR0", 0, C))
+    act(T.TB[:, TP:TP + C], row(0), F.Copy, runs("DR0", 0, C), ["P0"])
+
+    def result(m):
+        a, b = 128 * m, min(128 * m + 128, C)
+        quant_x(R, m)
+        mm(m, 128, T.QV[:, :], T.QVS[:, :], T.QX[:, a:a + 128], T.QXS[:, a:a + 128], ["QV", "QX%d" % m])
+        if m == 3:
+            for k in range(4):
+                dma("s" if k == 3 else "y", "sto%d" % (8 + k), T.osc[4 * k:4 * k + 4, :], T.QXS[32 * k:32 * k + 4, 0:C], ["QX%d" % i for i in range(4)], ["osc%d" % k])
+        act(T.YS[:, a:b], T.PS[:, 512 * m:512 * m + b - a], F.Copy, ["bk%d" % m], ["YS%d" % m])
+        if m:
+            a = 0 if m == 1 else a
+            ks = range(a // 128, m + 1)
+            dma("y", "sto%d" % m, T.oc[:, 4 * a:4 * b], T.QX[:, a:b].bitcast(dt.uint8), ["QX%d" % k for k in ks], ["oc%d" % m])
+            dma("s" if m == 3 else "y", "sto%d" % (4 + m), T.y[:, a:b], T.YS[:, a:b], ["YS%d" % k for k in ks], ["y%d" % m])
 
     for t in range(R):
-        lists(t)
+        lists()
         pointers(t)
         mosaic(t)
         join_list(t)
-        layer(t)
         if t == 0:
             quant(T.QV[:, :], T.QVS[:, :], T.VT[:, :], ["VT"], ["QV"])
-        join(t, 0)
+        if t == R - 1:
+            act(T.YO[:, :], row(R), F.Identity, runs("DR%d" % R, 0, C), ["YO"], bias=float(MID))
+            dma("y", "sto0", T.op[:, :], T.YO[0:128:16, :], ["YO"], ["op"])
+        for h in range(len(ZP)):
+            layer(t, h)
         if t < R - 1:
-            join(t, 1, [0])
-        quant_x(t + 1, 0)
-        if t < R - 1:
-            products(0)
-            scores_head()
-            join(t, 1, [1, 2])
-            runmax(0)
-            join(t, 1, [3])
-            runmax(1)
-            quant_x(t + 1, 1)
-            products(1)
+            join(t, 0, 128)
+            join(t, 128, 160)
+            score(t + 1, 0)
+            join(t, 160, 256)
+            before(0, 0, 128)
+            score(t + 1, 1)
+            join(t, 256, 384)
+            runmin(0, 2)
+            score(t + 1, 2)
+            join(t, 384, C)
+            before(1, 0, 128)
+            score(t + 1, 3)
+            before(1, 128, 256)
             scores_tail()
-    dma("y", "sto0", T.op[:, :], T.DR3[0:128:16, :], ["DR3"], ["op"])
-    dma("y", "sto1", T.oc[:, 0:1024], T.QX[:, 0:256].bitcast(dt.uint8), ["QXh0"], ["oc0"])
-    mm(6, 256, T.QV[:, :], T.QVS[:, :], T.QX[:, 0:256], T.QXS[:, 0:256], ["QV", "QXh0"])
-    act(T.YS[:, 0:256], T.PS[:, 3072:3328], F.Copy, ["bk6"], ["YS0"])
-    dma("y", "sto2", T.y[:, 0:256], T.YS[:, 0:256], ["YS0"], ["y0"])
-    join(R - 1, 1)
-    quant_x(R, 1)
-    mm(7, 192, T.QV[:, :], T.QVS[:, :], T.QX[:, 256:448], T.QXS[:, 256:448], ["QV", "QXh1"])
-    dma("y", "sto3", T.oc[:, 1024:1792], T.QX[:, 256:448].bitcast(dt.uint8), ["QXh1"], ["oc1"])
-    for k in range(4):
-        dma("s" if k % 2 else "y", "sto%d" % (5 + k), T.osc[4 * k:4 * k + 4, :], T.QXS[32 * k:32 * k + 4, 0:448], ["QXh0", "QXh1"], ["osc%d" % k])
-    vcopy(T.YS[:, 256:448], T.PS[:, 3584:3776], ["bk7"], ["YS1"])
-    dma("s", "sto4", T.y[:, 256:448], T.YS[:, 256:448], ["YS1"], ["y1"])
+        else:
+            join(t, 0, 128)
+            for m, (a, b) in enumerate(((128, 256), (256, 384), (384, C))):
+                join(t, a, b)
+                result(m)
+            result(3)
     kn = known["g"]
     for s in sorted(cnt):
         if kn.get(s, 0) < cnt[s]:

@@ -2,12 +2,13 @@ from concourse.mybir import dt, AluOpType as A, ActivationFunctionType as F
 
 C, R, N = 448, 3, 4
 MID = 224
-ZP = [(0, 128), (128, 288), (288, 448)]
-MOSAIC = [("pick", "v", 0, 128), ("pick", "s", 128, 288), ("pick", "s", 288, 448),
-          ("fold", 0, 128), ("four", 0, 128), ("part", "s", 48, 128), ("fold", 128, 288), ("part", "v", 0, 48), ("four", 128, 288),
-          ("part", "s", 184, 288), ("fold", 288, 448), ("pack", 0), ("four", 288, 448), ("part", "s", 360, 448), ("part", "v", 128, 184), ("pack", 1),
-          ("part", "v", 288, 360), ("pack", 2)]
+ZP = [(0, 128), (128, 304), (304, 448)]
+MOSAIC = [("pick", "v", 0, 64), ("pick", "s", 64, 128), ("pick", "v", 128, 224), ("pick", "s", 224, 448),
+          ("fold", 0, 128), ("fold", 128, 224), ("four", 0, 128), ("part", "s", 64, 128), ("four", 128, 224), ("part", "v", 0, 64),
+          ("fold", 224, 448), ("part", "s", 128, 224), ("pack", 0), ("four", 224, 448), ("part", "s", 352, 448), ("part", "v", 224, 304),
+          ("pack", 1), ("part", "v", 304, 352), ("pack", 2)]
 XL = [(0, 128), (128, 256), (256, 448)]
+JD = 384
 BIG = 1.0e29
 TP, TI, TS = 4 * C, 5 * C, 6 * C
 
@@ -19,7 +20,7 @@ def _b(n, t="float32"):
 BF, CODE, U8, U16, I32 = "bfloat16", "float8_e4m3fn_x4", "uint8", "uint16", "int32"
 SCRATCH = {
     "PS": ("psum", [128, 4096], "float32"),
-    "UT": _b(512, BF), "VT": _b(512, BF), "Z": _b(1792, BF), "THR": _b(128, BF),
+    "X": _b(2048, BF), "JG": _b(4 * (C - JD)), "UT": _b(512, BF), "VT": _b(512, BF), "Z": _b(1792, BF), "THR": _b(128, BF),
     "SG": _b(1792, BF), "CM": _b(1792, BF), "SCN": _b(1968, BF),
     "TT": _b(32, BF), "LT0": _b(32, BF), "LT1": _b(32, BF), "LR": _b(64, BF),
     "QU": _b(128, CODE), "QUS": _b(128, U8), "QU1": _b(144, CODE), "QU1S": _b(144, U8), "QV": _b(128, CODE), "QVS": _b(128, U8),
@@ -36,15 +37,13 @@ for _i in ("RK", "RK1", "OL", "PL"):
     SCRATCH[_i] = _b(28, U16)
 for _i in ("A16", "JW", "y1", "y2", "y3", "r1", "wf", "lm", "o1", "o2"):
     SCRATCH[_i] = _b(28)
-for _i in range(4):
-    SCRATCH["X%d" % _i] = _b(2048, BF)
 for _i in range(R):
     for _n in ("QZ", "LZ"):
         SCRATCH["%s%d" % (_n, _i)] = _b(448, CODE)
         SCRATCH["%sS%d" % (_n, _i)] = _b(448, U8)
 
 SEMAPHORES = ["sv", "ss", "st", "sg", "loc"]
-SEMAPHORES += ["ld%d" % _i for _i in range(8)] + ["sto%d" % _i for _i in range(12)]
+SEMAPHORES += ["ld%d" % _i for _i in range(8)] + ["ga%d" % _i for _i in range(R - 1)] + ["sto%d" % _i for _i in range(12)]
 SEMAPHORES += ["ar%d%d" % (_t, _h) for _t in range(R) for _h in range(len(ZP))]
 
 
@@ -96,9 +95,9 @@ def rank_program(g, core, T, topo):
         fn(*args, **kw).then_inc(T.sem[s], 1)
         note(qn, reads, writes, s, n, False)
 
-    def dma(qn, s, out, in_, reads, writes):
+    def dma(qn, s, out, in_, reads, writes, **kw):
         waits(qn, reads, writes)
-        q[qn].dma_start(out, in_).then_inc(T.sem[s], 16)
+        q[qn].dma_start(out, in_, **kw).then_inc(T.sem[s], 16)
         cnt[s] = 16
         note(qn, reads, writes, s, 16, True)
 
@@ -146,20 +145,18 @@ def rank_program(g, core, T, topo):
 
     dma("s", "ld0", T.UT[:, :], T.u[:, :], [], ["UT"])
     for i, (a, b) in enumerate(XL):
-        dma("y", "ld%d" % (1 + i), T.X0[:, 4 * a:4 * b], T.x[:, 4 * a:4 * b], [], runs("X0", a, b))
+        dma("y", "ld%d" % (1 + i), T.X[:, 4 * a:4 * b], T.x[:, 4 * a:4 * b], [], runs("X", a, b))
     dma("s", "ld4", T.PI[:, :], T.p[:, :], [], ["PI"])
     dma("y", "ld5", T.WC[:, :].bitcast(dt.uint8), T.wc[:, :], [], ["WC"])
-    dma("y", "ld6", T.WS[:, :], T.ws[:, :], [], ["WS"])
     dma("y", "ld7", T.VT[:, :], T.v[:, :], [], ["VT"])
 
     iota(T.PIX[:, :], [[0, 1]], "PIX", 1, False)
     iota(T.MD[:, :], [[0, 112], [1, 4]], "MD")
     iota(T.TB[:, TI:TI + C], [[1, C]], "IO", base=-MID)
     iota(T.A16[:, :], [[16, 28]], "A16")
-    for t in range(1, R + 1):
-        iota(T["X%d" % t][:, 4 * C:2048], [[0, 256]], "X%dz" % t)
+    dma("g", "ld6", T.WS[:, :], T.ws[:, :], [], ["WS"])
     fill(T.U1L[:, :], 1, "U1L")
-    fill(T.X0[:, 4 * C:2048], 0.0, "X0z")
+    do("v", V.memset, (T.X[:, 4 * C:2048], 0.0), [], runs("X", C, 512))
     fill(T.Z2[:, :], 0.0, "Z2")
     ts(T.PMI[:, :], T.PIX[:, :], 15, None, [A.bitwise_and], ["PIX"], ["PMI"])
     ts(T.GI[:, :], T.PIX[:, :], 4, None, [A.arith_shift_right], ["PIX"], ["GI"])
@@ -180,7 +177,6 @@ def rank_program(g, core, T, topo):
     fill(T.TT[:, :], 0.0, "TT")
     tt(T.PO[:, :], T.u1[:, :], T.PE[:, :], A.add, ["u1", "PE"], ["PO"])
     ts(T.YO[:, :], T.MD[:, :], T.PQ[:, 0:1], 8704.0, [A.is_gt, A.mult], ["MD", "PQ"], ["YO"])
-    act(T.MASK[:, :], T.YO[:, :], F.Identity, ["YO"], ["MASK"], bias=-8192.0)
 
     def late_constants():
         ts(T.THR[:, :], T.TB[:, TI:TI + 128], T.PF[:, 0:1], 0.5, [A.is_gt, A.subtract], ["IO", "PF"], ["THR"])
@@ -188,21 +184,25 @@ def rank_program(g, core, T, topo):
             ts(T["DUP%d" % e][:, :], T.Z2[:, 0:2], T.PM[:, 0:1], 16.0 * e, [A.add, A.add], ["Z2", "PM"], ["DUP%d" % e])
         ts(T.JW[:, :], T.A16[:, :], T.PM[:, 0:1], None, [A.add], ["A16", "PM"], ["JW"])
 
-    def quant_x(t, m):
+    def quant_x(m):
         a = 128 * m
-        quant(T.QX[:, a:a + 128], T.QXS[:, a:a + 128], T["X%d" % t][:, 4 * a:4 * a + 512],
-              runs("X%d" % t, a, min(a + 128, C)) + (["X%dz" % t] if m == 3 else []), ["QX%d" % m])
+        quant(T.QX[:, a:a + 128], T.QXS[:, a:a + 128], T.X[:, 4 * a:4 * a + 512], runs("X", a, a + 128), ["QX.%d" % m])
 
     UK = ["QU1c", "QU1s"]
     ROWS = [4, 5, 6, 7]
 
-    def products(m):
+    def products(m, straight):
         a = 128 * m
-        mm(m % 2, 128, T.QX[:, a:a + 128], T.QXS[:, a:a + 128], T.QU1[:, 0:128], T.QU1S[:, 0:128], ["QX%d" % m] + UK)
-        lo = a if m == 3 else 0
-        for bank in [ROWS[m]] + ([2] if m == 3 else []):
-            mm(bank, a + 128 - lo, T.QU1[:, 16:144], T.QU1S[:, 16:144], T.QX[:, lo:a + 128], T.QXS[:, lo:a + 128],
-               ["QX%d" % k for k in range(lo // 128, m + 1)] + UK)
+
+        def line(bank, lo, hi):
+            mm(bank, hi - lo, T.QU1[:, 16:144], T.QU1S[:, 16:144], T.QX[:, lo:hi], T.QXS[:, lo:hi], runs("QX", lo, hi, 128) + UK)
+
+        if straight:
+            line(3, 0, a)
+        mm(m % 2, 128, T.QX[:, a:a + 128], T.QXS[:, a:a + 128], T.QU1[:, 0:128], T.QU1S[:, 0:128], ["QX.%d" % m] + UK)
+        if m == 3:
+            line(2, a, a + 128)
+        line(ROWS[m], a if m == 3 else 0, a + 128)
 
     def negs(m):
         act(T.NB[:, 10 * m:10 * m + 10], T.PS[:, 512 * (m % 2):512 * (m % 2) + 10], F.Copy, ["bk%d" % (m % 2)], ["NB%d" % m], scale=-1.0)
@@ -212,17 +212,16 @@ def rank_program(g, core, T, topo):
         act(T.SG[:, C * m + a:C * m + b], T.PS[:, o + a:o + b], F.Sign, ["bk%d" % ROWS[k], "NB%d" % m], runs("SG%d" % m, a, b, 128),
             bias=T.NB[:, 10 * m + 9:10 * m + 10])
 
-    def signs(k):
+    def signs(k, straight):
         negs(k)
         if k == 3:
+            sign(1, 256, 384, 2)
             sign(3, 0, 384, 2)
             sign(3, 384, C, 3)
             return
-        if k == 2:
-            level(0); level(1)
-        sign(k, 0, 128 * k + 128, k)
-        for m in range(k):
-            sign(m, 128 * k, 128 * k + 128, k)
+        if k:
+            sign(0, 128 * k, 128 * k + 128, k)
+        sign(k, 128 * k if straight else 0, 128 * k + 128, k)
 
     def runmin(a, b):
         scan(T.RUN[:, 10 * a:10 * b], T.RS[:, 10 * a:10 * b], T.NB[:, 10 * a:10 * b], 0.0, A.add, A.min,
@@ -249,17 +248,20 @@ def rank_program(g, core, T, topo):
         scan(T.SCN[:, 224 * m:224 * m + 224], T.CM[:, o:o + 224], T.CM[:, o + 224:o + C], -225.0, A.add, A.add,
              runs("CM%d" % m, 0, C, 128), ["SCN%d" % m])
 
-    def scores_tail():
-        before(2, 0, 256)
+    def scores_tail(straight):
+        if straight:
+            ts(T.CM[:, 2 * C:2 * C + 256], T.PS[:, 1536:1792], T.NB[:, 29:30], 0.0, [A.add, A.is_ge], ["bk3", "NB2"], runs("CM2", 0, 256, 128))
+        before(0, 128, 384)
         last_run(0); last_run(1); last_run(2)
+        count(0)
+        if not straight:
+            before(2, 0, 256)
         before(2, 256, 384)
         runmin(2, 4)
         level(2); level(3)
-        before(0, 128, 384)
         before(1, 256, 384)
         count(2)
         ts(T.CF[:, :], T.NB[:, 8:40:10], 0.0, 16.0, [A.is_lt, A.mult], ["NB0", "NB1", "NB2", "NB3"], ["CF"])
-        count(0)
         before(3, 0, 384)
         before(3, 384, C)
         count(1)
@@ -272,10 +274,10 @@ def rank_program(g, core, T, topo):
     def lists():
         rd = ["SCN0", "SCN1", "SCN2", "SCN3", "SCNw"]
         for b in range(1, 4):
-            vcopy(T.SCN[0:32, 223 + 56 * b:1968:224], T.SCN[32 * b:32 * b + 32, 223:1792:224], rd, ["NAT%d" % b])
+            move("vvs"[b - 1], T.SCN[0:32, 223 + 56 * b:1968:224], T.SCN[32 * b:32 * b + 32, 223:1792:224], rd, ["NAT%d" % b])
         do("v", V.transpose, (T.TT[0:32, 0:32], T.SCN[0:32, 223:1968:56]), rd + ["NAT1", "NAT2", "NAT3"], ["TT"])
         for e in range(2):
-            vcopy(T["LT%d" % e][:, :], T.TT[:, 0:32].indirect(T["DUP%d" % e][:, 0:2]), ["TT", "DUP%d" % e], ["LT%d" % e])
+            move("vs"[e], T["LT%d" % e][:, :], T.TT[:, 0:32].indirect(T["DUP%d" % e][:, 0:2]), ["TT", "DUP%d" % e], ["LT%d" % e])
         for e in range(2):
             do("v", V.transpose, (T.LR[0:32, e:64:2], T["LT%d" % e][0:32, 0:32]), ["LT%d" % e], ["LRe%d" % e])
         for b in range(4):
@@ -299,6 +301,9 @@ def rank_program(g, core, T, topo):
         act(T.y2[:, :], T.y1[:, :], F.Abs, ["y1"], ["y2"], bias=-(d + 15 * s) / 2, scale=float(s))
         act(T.wf[:, :], T.LR[:, 0:28], F.Relu, LRK, ["wf"], bias=-222.0 * C, scale=float(C))
         act(T.y3[:, :], T.y2[:, :], F.Relu, ["y2"], ["y3"], bias=-(15 * s - d) / 2)
+        if t == 0:
+            act(T.TB[:, TP:TP + C], row(0), F.Copy, runs("DR0", 0, C), ["P0"])
+            act(T.MASK[:, :], T.YO[:, :], F.Identity, ["YO"], ["MASK"], bias=-8192.0)
         sort(T.TB[:, TS:TS + C], t, 0, 288, "TBs")
         tt(T.o1[:, :], T.y3[:, :], T.JW[:, :], A.add, ["y3", "JW"], ["o1"])
         tt(T.lm[:, :], T.r1[:, :], T.wf[:, :], A.subtract, ["r1", "wf"], ["lm"])
@@ -326,8 +331,7 @@ def rank_program(g, core, T, topo):
 
     def mosaic(t):
         def part(qn, a, b):
-            move(qn, T.Z[:, 4 * a:4 * b], T["X%d" % t][:, 0:4 * C].indirect(T.OF[:, a // 4:b // 4]),
-                 runs("X%d" % t, 0, C) + runs("OF", a, b), runs("Z", a, b, 8))
+            move(qn, T.Z[:, 4 * a:4 * b], T.X[:, 0:4 * C].indirect(T.OF[:, a // 4:b // 4]), runs("X", 0, C) + runs("OF", a, b), runs("Z", a, b, 8))
 
         def pack(h):
             a, b = ZP[h]
@@ -348,14 +352,14 @@ def rank_program(g, core, T, topo):
 
     def join_list(t):
         sort(T.PD[:, 0:C], t + 1, 0, C, "PD")
-        for h, qn in enumerate("vv"):
+        layer(t, 0)
+        for h, qn in enumerate("vs"):
             a, b = 224 * h, 224 * h + 224
             move(qn, T.VR[:, a:b], T.PD[:, 0:C].indirect(T.RK1[:, a // 16:b // 16]), ["PD", "RK1"], runs("VR", a, b))
         for h in range(2):
             a, b = 224 * h, 224 * h + 224
             fold(T.VR[:, a:b], runs("VR", a, b), a, b)
-        for h in range(2):
-            four("EL", 224 * h, 224 * h + 224)
+        four("EL", 0, 224)
 
     def layer(t, h):
         a, b = ZP[h]
@@ -373,45 +377,47 @@ def rank_program(g, core, T, topo):
 
     HK = ["HS%dh%d" % (w, h) for w in range(4) for h in range(len(ZP))]
 
-    def join(t, a, b):
-        tt(T["X%d" % (t + 1)][:, 4 * a:4 * b], T.HS[:, 0:4 * C].indirect(T.EL[:, a // 4:b // 4]), T["X%d" % t][:, 4 * a:4 * b], A.add,
-           HK + runs("EL", a, b) + runs("X%d" % t, a, b), runs("X%d" % (t + 1), a, b))
+    def join(a, b):
+        tt(T.X[:, 4 * a:4 * b], T.HS[:, 0:4 * C].indirect(T.EL[:, a // 4:b // 4]), T.X[:, 4 * a:4 * b], A.add,
+           HK + runs("EL", a, b) + runs("X", a, b), runs("X", a, b))
 
-    def score(t, m):
-        quant_x(t, m)
-        products(m)
-        signs(m)
+    def join_by_dma(t, a, b):
+        act(T.JG[:, 0:4 * (b - a)], T.HS[:, 0:4 * C].indirect(T.EL[:, a // 4:b // 4]), F.Copy, HK + runs("EL", a, b), ["JG"])
+        dma("g", "ga%d" % t, T.X[:, 4 * a:4 * b], T.JG[:, 0:4 * (b - a)], ["JG"] + runs("X", a, b), runs("X", a, b), accum_op=A.add)
+
+    def score(m, straight=False):
+        quant_x(m)
+        products(m, straight)
+        signs(m, straight)
 
     quant(T.QU[:, :], T.QUS[:, :], T.UT[:, :], ["UT"], ["QU"])
     vcopy(T.QU1[:, :].bitcast(dt.uint32), T.QU[:, 0:128].bitcast(dt.uint32).indirect(T.U1L[:, 0:9]), ["QU", "U1L"], ["QU1c"])
     act(T.QU1S[:, :], T.QUS[:, 0:128].indirect(T.U1L[:, 0:9]), F.Copy, ["QU", "U1L"], ["QU1s"])
-    score(0, 0)
+    score(0)
     late_constants()
-    score(0, 1)
+    score(1)
     vcopy(T.PL[:, :], T.PI[:, :], ["PI"], ["PL"])
     before(0, 0, 128)
     runmin(0, 2)
-    score(0, 2)
-    score(0, 3)
+    level(0); level(1)
+    score(2, True)
+    score(3)
     before(1, 0, 128)
     before(1, 128, 256)
-    scores_tail()
+    scores_tail(True)
     act(row(0), T.TB[:, TI:TI + C].indirect(T.PL[:, 0:28]), F.Copy, ["IO", "PL"], runs("DR0", 0, C))
-    act(T.TB[:, TP:TP + C], row(0), F.Copy, runs("DR0", 0, C), ["P0"])
 
-    def result(m):
-        a, b = 128 * m, min(128 * m + 128, C)
-        quant_x(R, m)
-        mm(m, 128, T.QV[:, :], T.QVS[:, :], T.QX[:, a:a + 128], T.QXS[:, a:a + 128], ["QV", "QX%d" % m])
-        if m == 3:
-            for k in range(4):
-                dma("s" if k == 3 else "y", "sto%d" % (8 + k), T.osc[4 * k:4 * k + 4, :], T.QXS[32 * k:32 * k + 4, 0:C], ["QX%d" % i for i in range(4)], ["osc%d" % k])
-        act(T.YS[:, a:b], T.PS[:, 512 * m:512 * m + b - a], F.Copy, ["bk%d" % m], ["YS%d" % m])
-        if m:
-            a = 0 if m == 1 else a
-            ks = range(a // 128, m + 1)
-            dma("y", "sto%d" % m, T.oc[:, 4 * a:4 * b], T.QX[:, a:b].bitcast(dt.uint8), ["QX%d" % k for k in ks], ["oc%d" % m])
-            dma("s" if m == 3 else "y", "sto%d" % (4 + m), T.y[:, a:b], T.YS[:, a:b], ["YS%d" % k for k in ks], ["y%d" % m])
+    def result(a, b):
+        m = a // 128
+        quant(T.QX[:, a:b], T.QXS[:, a:b], T.X[:, 4 * a:4 * b], runs("X", a, b), runs("QX", a, b, 128))
+        if b > 128:
+            lo = a if b == C else 0
+            dma("y", "sto%d" % (4 + m), T.oc[:, 4 * lo:4 * b], T.QX[:, lo:b].bitcast(dt.uint8), runs("QX", lo, b, 128), ["oc%d" % m])
+        mm(m, b - a, T.QV[:, :], T.QVS[:, :], T.QX[:, a:b], T.QXS[:, a:b], ["QV"] + runs("QX", a, b, 128))
+        move("v" if b == C else "s", T.YS[:, a:b], T.PS[:, 512 * m:512 * m + b - a], ["bk%d" % m], runs("YS", a, b, 128))
+
+    def store(qn, i, a, b):
+        dma(qn, "sto%d" % i, T.y[:, a:b], T.YS[:, a:b], runs("YS", a, b, 128), ["y%d" % i])
 
     for t in range(R):
         lists()
@@ -420,32 +426,42 @@ def rank_program(g, core, T, topo):
         join_list(t)
         if t == 0:
             quant(T.QV[:, :], T.QVS[:, :], T.VT[:, :], ["VT"], ["QV"])
+        for h in range(1, len(ZP)):
+            layer(t, h)
+        four("EL", 224, C)
         if t == R - 1:
             act(T.YO[:, :], row(R), F.Identity, runs("DR%d" % R, 0, C), ["YO"], bias=float(MID))
             dma("y", "sto0", T.op[:, :], T.YO[0:128:16, :], ["YO"], ["op"])
-        for h in range(len(ZP)):
-            layer(t, h)
         if t < R - 1:
-            join(t, 0, 128)
-            join(t, 128, 160)
-            score(t + 1, 0)
-            join(t, 160, 256)
+            join(0, 128)
+            join(128, 160)
+            score(0)
+            join(160, 256)
+            join(256, 288)
+            score(1)
+            join(288, JD)
             before(0, 0, 128)
-            score(t + 1, 1)
-            join(t, 256, 384)
+            quant_x(2)
             runmin(0, 2)
-            score(t + 1, 2)
-            join(t, 384, C)
+            level(0); level(1)
+            products(2, True)
+            signs(2, True)
+            join(JD, C)
             before(1, 0, 128)
-            score(t + 1, 3)
+            score(3)
             before(1, 128, 256)
-            scores_tail()
-        else:
-            join(t, 0, 128)
-            for m, (a, b) in enumerate(((128, 256), (256, 384), (384, C))):
-                join(t, a, b)
-                result(m)
-            result(3)
+            scores_tail(True)
+    join(0, 128)
+    join(128, 256)
+    result(0, 128)
+    join(256, 352)
+    result(128, 256)
+    store("y", 1, 0, 256)
+    join(352, C)
+    result(256, C)
+    for k in range(4):
+        dma("s" if k > 1 else "y", "sto%d" % (8 + k), T.osc[4 * k:4 * k + 4, :], T.QXS[32 * k:32 * k + 4, 0:C], runs("QX", 0, C, 128), ["osc%d" % k])
+    store("s", 2, 256, C)
     kn = known["g"]
     for s in sorted(cnt):
         if kn.get(s, 0) < cnt[s]:

@@ -7,6 +7,20 @@ MOSAIC = [("pick", "v", 0, 64), ("pick", "s", 64, 128), ("pick", "v", 128, 224),
           ("fold", 0, 128), ("fold", 128, 224), ("four", 0, 128), ("part", "s", 64, 128), ("four", 128, 224), ("part", "v", 0, 64),
           ("fold", 224, 448), ("part", "s", 128, 224), ("pack", 0), ("four", 224, 448), ("part", "s", 352, 448), ("part", "v", 224, 304),
           ("pack", 1), ("part", "v", 304, 352), ("pack", 2)]
+TAIL = [("direct", 2, 0, 256, 3), ("before", 0, 128, 384), ("direct", 0, 384, C, 2), ("direct", 1, 384, C, 2), ("direct", 2, 384, C, 2), ("count", 0),
+        ("before", 2, 256, 384), ("runmin", 2, 4), ("level", 2), ("level", 3), ("before", 1, 256, 384), ("count", 2), ("calls",),
+        ("before", 3, 0, 384), ("before", 3, 384, C), ("count", 1), ("count", 3), ("kinds",)]
+RUN0 = [("quant", 0), ("cols", 0), ("line", 4, 0, 128), ("negs", 0), ("sign", 0, 0, 128, 4)]
+RUN1 = [("quant", 1), ("cols", 1), ("line", 5, 0, 256), ("line", 3, 0, 256), ("negs", 1), ("sign", 0, 128, 256, 5), ("sign", 1, 0, 256, 5)]
+RUN2 = [("cols", 2), ("line", 6, 256, 384), ("negs", 2), ("sign", 0, 256, 384, 6), ("sign", 2, 256, 384, 6)]
+RUN3 = [("quant", 3), ("cols", 3), ("line", 2, 384, 512), ("line", 7, 256, C), ("negs", 3), ("sign", 1, 256, 384, 6), ("sign", 3, 0, 256, 5), ("sign", 3, 256, C, 7)]
+START = (RUN0 + [("places", 1), ("late",)] + RUN1
+         + [("places", 2), ("first",), ("places", 5), ("places", 3), ("before", 0, 0, 128), ("places", 4), ("runmin", 0, 2), ("level", 0), ("level", 1), ("quant", 2)]
+         + RUN2 + RUN3 + [("before", 1, 0, 128), ("before", 1, 128, 256)] + TAIL)
+JOIN = ([("join", 0, 128), ("join", 128, 160)] + RUN0 + [("join", 160, 256), ("join", 256, 288)] + RUN1
+        + [("join", 288, 384), ("before", 0, 0, 128), ("quant", 2), ("runmin", 0, 2), ("level", 0), ("level", 1)] + RUN2
+        + [("join", 384, C), ("before", 1, 0, 128)] + RUN3 + [("before", 1, 128, 256)] + TAIL)
+HALVED = []
 XL = [(0, 128), (128, 256), (256, 448)]
 JD = 384
 BIG = 1.0e29
@@ -21,22 +35,28 @@ BF, CODE, U8, U16, I32 = "bfloat16", "float8_e4m3fn_x4", "uint8", "uint16", "int
 SCRATCH = {
     "PS": ("psum", [128, 4096], "float32"),
     "X": _b(2048, BF), "JG": _b(4 * (C - JD)), "UT": _b(512, BF), "VT": _b(512, BF), "Z": _b(1792, BF), "THR": _b(128, BF),
-    "SG": _b(1792, BF), "CM": _b(1792, BF), "SCN": _b(1968, BF),
-    "TT": _b(32, BF), "LT0": _b(32, BF), "LT1": _b(32, BF), "LR": _b(64, BF),
+    "SG": _b(1792, BF), "CM": _b(1792, BF), "SCN": _b(7168, BF),
+    "TRI": _b(384, BF), "TRJ": _b(128, BF), "WA": _b(3), "IN": _b(3), "TT": _b(160, BF),
     "QU": _b(128, CODE), "QUS": _b(128, U8), "QU1": _b(144, CODE), "QU1S": _b(144, U8), "QV": _b(128, CODE), "QVS": _b(128, U8),
     "WC": _b(512, CODE), "WS": _b(512, U8), "QX": _b(512, CODE), "QXS": _b(512, U8),
     "PI": _b(28, I32), "PIX": _b(1, I32), "PMI": _b(1, I32), "GI": _b(1, I32), "PQI": _b(1, I32), "PEI": _b(1, I32),
-    "DUP0": _b(2, U16), "DUP1": _b(2, U16), "U1L": _b(10, U16), "OF": _b(112, U16), "EL": _b(112, U16),
+    "Q2I": _b(1, I32), "H2I": _b(1, I32), "Q2": _b(1), "H2": _b(1), "LK": _b(2, U16), "LC": _b(2, U16), "PL": _b(28, U16), "U1L": _b(10, U16), "OF": _b(112, U16), "EL": _b(112, U16),
     "TB": _b(7 * C, BF), "PD": _b(448, BF), "VR": _b(448, BF), "SC": _b(448, "float16"), "MASK": _b(448, BF),
     "MD": _b(448), "HS": _b(1792), "YS": _b(448), "YO": _b(448),
-    "Z2": _b(2), "NB": _b(40), "RS": _b(40), "RUN": _b(40), "LJ": _b(32), "LV": _b(4), "CF": _b(4),
+    "NB": _b(40), "RS": _b(40), "RUN": _b(40), "LJ": _b(32), "LV": _b(4), "CF": _b(4),
 }
 for _i in ("PM", "PF", "NG", "PQ", "PE", "PO", "u1", "u2", "u3"):
     SCRATCH[_i] = _b(1)
-for _i in ("RK", "RK1", "OL", "PL"):
-    SCRATCH[_i] = _b(28, U16)
-for _i in ("A16", "JW", "y1", "y2", "y3", "r1", "wf", "lm", "o1", "o2"):
-    SCRATCH[_i] = _b(28)
+for _i in ("RK", "RK1", "OL"):
+    SCRATCH[_i] = _b(32, U16)
+for _i in ("A16", "JW", "y1", "y2"):
+    SCRATCH[_i] = _b(32)
+for _i in ("MA", "MB", "MO"):
+    SCRATCH[_i] = _b(128)
+for _i in ("k0", "k1", "k2", "km", "kd", "kb", "ke"):
+    SCRATCH[_i] = _b(2, I32)
+for _i in ("c1", "c2", "c3", "cs", "ca", "cb", "cd", "ce", "cp", "c4", "cc"):
+    SCRATCH[_i] = _b(2)
 for _i in range(R):
     for _n in ("QZ", "LZ"):
         SCRATCH["%s%d" % (_n, _i)] = _b(448, CODE)
@@ -147,81 +167,92 @@ def rank_program(g, core, T, topo):
     for i, (a, b) in enumerate(XL):
         dma("y", "ld%d" % (1 + i), T.X[:, 4 * a:4 * b], T.x[:, 4 * a:4 * b], [], runs("X", a, b))
     dma("s", "ld4", T.PI[:, :], T.p[:, :], [], ["PI"])
+    waits("y", runs("X", 0, C), [])
     dma("y", "ld5", T.WC[:, :].bitcast(dt.uint8), T.wc[:, :], [], ["WC"])
+    dma("y", "ld6", T.WS[:, :], T.ws[:, :], [], ["WS"])
     dma("y", "ld7", T.VT[:, :], T.v[:, :], [], ["VT"])
 
     iota(T.PIX[:, :], [[0, 1]], "PIX", 1, False)
+    iota(T.A16[:, :], [[16, 32]], "A16")
     iota(T.MD[:, :], [[0, 112], [1, 4]], "MD")
     iota(T.TB[:, TI:TI + C], [[1, C]], "IO", base=-MID)
-    iota(T.A16[:, :], [[16, 28]], "A16")
-    dma("g", "ld6", T.WS[:, :], T.ws[:, :], [], ["WS"])
+    iota(T.SCN[:, 896:1792], [[0, 896]], "SCNy")
     fill(T.U1L[:, :], 1, "U1L")
     do("v", V.memset, (T.X[:, 4 * C:2048], 0.0), [], runs("X", C, 512))
-    fill(T.Z2[:, :], 0.0, "Z2")
-    ts(T.PMI[:, :], T.PIX[:, :], 15, None, [A.bitwise_and], ["PIX"], ["PMI"])
-    ts(T.GI[:, :], T.PIX[:, :], 4, None, [A.arith_shift_right], ["PIX"], ["GI"])
-    vcopy(T.PM[:, :], T.PMI[:, :], ["PMI"], ["PM"])
-    ts(T.u1[:, :], T.PMI[:, :], 16.0, -1.0, [A.mult, A.add], ["PMI"], ["u1"])
-    ts(T.PF[:, :], T.PIX[:, :], -float(MID), None, [A.add], ["PIX"], ["PF"])
-    ts(T.u2[:, :], T.PM[:, :], 8.0, T.u1[:, 0:1], [A.is_lt, A.mult], ["PM", "u1"], ["u2"])
-    ts(T.PQI[:, :], T.PMI[:, :], 2, None, [A.arith_shift_right], ["PMI"], ["PQI"])
-    ts(T.u3[:, :], T.PM[:, :], 8.0, T.u2[:, 0:1], [A.is_equal, A.add], ["PM", "u2"], ["u3"])
-    ts(T.PEI[:, :], T.PIX[:, :], 3, None, [A.bitwise_and], ["PIX"], ["PEI"])
-    ts(T.U1L[:, 0:1], T.u3[:, :], 1.0, None, [A.add], ["u3", "U1L"], ["U1L"])
-    vcopy(T.PQ[:, :], T.PQI[:, :], ["PQI"], ["PQ"])
-    vcopy(T.PE[:, :], T.PEI[:, :], ["PEI"], ["PE"])
     fill(T.RS[:, :], 0.0, "RS")
-    ts(T.NG[:, :], T.GI[:, :], -1.0, None, [A.mult], ["GI"], ["NG"])
+
+    def c1(o, a, s1, s2, *ops):
+        col = [s for s in (s1, s2) if s in SCRATCH]
+        n = SCRATCH[o][1][1]
+        ts(T[o][:, 0:n], T[a][:, 0:n], T[s1][:, 0:1] if s1 in col else s1, T[s2][:, 0:1] if s2 in col else s2, ops, [a] + col, [o])
+
+    def c2(o, a, b, op):
+        tt(T[o][:, :], T[a][:, :], T[b][:, :], op, [a, b], [o])
+
+    SHR, AND = A.arith_shift_right, A.bitwise_and
+    c1("PMI", "PIX", 15, None, AND); c1("PQI", "PIX", 2, 3, SHR, AND); c1("Q2I", "PIX", 4, 6, SHR, AND); c1("H2I", "PIX", 3, 2, SHR, AND)
+    c1("PM", "PMI", 0.0, None, A.add); c1("u1", "PMI", 16.0, -1.0, A.mult, A.add); c1("PQ", "PQI", -1.0, -0.5, A.mult, A.add); c1("PF", "PIX", -float(MID), None, A.add)
+    c1("u2", "PM", 8.0, "u1", A.is_lt, A.mult); c1("JW", "A16", "PM", None, A.add); c1("Q2", "Q2I", 0.0, None, A.add); c1("H2", "H2I", 0.0, None, A.add)
+    c1("u3", "PM", 8.0, "u2", A.is_equal, A.add)
+    c1("k0", "JW", 0.0, None, A.add); c1("k1", "JW", "Q2", 8.0, A.subtract, A.add); c1("k2", "JW", "H2", 8.0, A.subtract, A.add)
+    ts(T.U1L[:, 0:1], T.u3[:, :], 1.0, None, [A.add], ["u3", "U1L"], ["U1L"])
+    c1("km", "k0", 3, None, SHR); c1("ke", "k0", 1, None, AND); c1("kd", "k1", 1, 3, SHR, AND); c1("kb", "k2", 1, 3, SHR, AND)
     fill(T.RS[:, 0:40:10], BIG, "RS")
-    ts(T.u1[:, :], T.PQ[:, :], 2048.0, 4.0 * MID - 3 * 2048, [A.mult, A.add], ["PQ"], ["u1"])
-    fill(T.TT[:, :], 0.0, "TT")
-    tt(T.PO[:, :], T.u1[:, :], T.PE[:, :], A.add, ["u1", "PE"], ["PO"])
-    ts(T.YO[:, :], T.MD[:, :], T.PQ[:, 0:1], 8704.0, [A.is_gt, A.mult], ["MD", "PQ"], ["YO"])
+    c1("c1", "km", 224.0, 223.0, A.mult, A.add); c1("c2", "kd", -56.0, None, A.mult)
+    c1("c3", "kb", 32.0, 1792.0, A.mult, A.add); c1("cs", "ke", 2.0, "H2", A.mult, A.is_equal)
+    act(T.YO[:, :], T.MD[:, :], F.Sign, ["MD", "PQ"], ["YO"], bias=T.PQ[:, 0:1])
 
     def late_constants():
         ts(T.THR[:, :], T.TB[:, TI:TI + 128], T.PF[:, 0:1], 0.5, [A.is_gt, A.subtract], ["IO", "PF"], ["THR"])
-        for e in range(2):
-            ts(T["DUP%d" % e][:, :], T.Z2[:, 0:2], T.PM[:, 0:1], 16.0 * e, [A.add, A.add], ["Z2", "PM"], ["DUP%d" % e])
-        ts(T.JW[:, :], T.A16[:, :], T.PM[:, 0:1], None, [A.add], ["A16", "PM"], ["JW"])
+
+    def places(i):
+        if i == 0:
+            c2("ca", "c1", "c2", A.add); c2("cb", "c3", "km", A.add)
+        elif i == 1:
+            c2("cd", "ca", "cb", A.subtract); c1("c4", "cs", 892.0, 4.0, A.mult, A.add)
+        elif i == 2:
+            c2("ce", "cd", "cs", A.mult)
+        elif i == 3:
+            c2("cp", "cb", "ce", A.add)
+        elif i == 4:
+            c2("cc", "cp", "c4", A.add)
+        elif i == 5:
+            fill(T.SCN[:, 2015:7168:224], 0.0, "SCNz")
+        elif i == 6:
+            c1("LK", "cp", 0.0, None, A.add); c1("LC", "cc", 0.0, None, A.add); c1("GI", "PIX", 4, None, SHR)
+        elif i == 7:
+            c1("NG", "GI", -1.0, None, A.mult); c1("PEI", "PIX", 3, None, AND)
+            fill(T.MB[:, 3:128:4], 65536.0, "MB")
+        elif i == 8:
+            fill(T.MA[:, 0:128:4], 65536.0, "MA0"); fill(T.MA[:, 1:128:4], 0.0, "MA1")
+            c1("u1", "PQI", 2048.0, 4.0 * MID - 3 * 2048, A.mult, A.add)
+        else:
+            ts(T.MA[:, 2:128:4], T.JW[:, :], -1.0, None, [A.mult], ["JW"], ["MA2"]); vcopy(T.MA[:, 3:128:4], T.JW[:, :], ["JW"], ["MA3"])
+            c1("PO", "PEI", "u1", None, A.add)
 
     def quant_x(m):
         a = 128 * m
         quant(T.QX[:, a:a + 128], T.QXS[:, a:a + 128], T.X[:, 4 * a:4 * a + 512], runs("X", a, a + 128), ["QX.%d" % m])
 
     UK = ["QU1c", "QU1s"]
-    ROWS = [4, 5, 6, 7]
 
-    def products(m, straight):
+    first = {}
+
+    def cols(m):
         a = 128 * m
-
-        def line(bank, lo, hi):
-            mm(bank, hi - lo, T.QU1[:, 16:144], T.QU1S[:, 16:144], T.QX[:, lo:hi], T.QXS[:, lo:hi], runs("QX", lo, hi, 128) + UK)
-
-        if straight:
-            line(3, 0, a)
         mm(m % 2, 128, T.QX[:, a:a + 128], T.QXS[:, a:a + 128], T.QU1[:, 0:128], T.QU1S[:, 0:128], ["QX.%d" % m] + UK)
-        if m == 3:
-            line(2, a, a + 128)
-        line(ROWS[m], a if m == 3 else 0, a + 128)
+
+    def line(bank, a, b):
+        first[bank] = a
+        mm(bank, b - a, T.QU1[:, 16:144], T.QU1S[:, 16:144], T.QX[:, a:b], T.QXS[:, a:b], runs("QX", a, b, 128) + UK)
 
     def negs(m):
         act(T.NB[:, 10 * m:10 * m + 10], T.PS[:, 512 * (m % 2):512 * (m % 2) + 10], F.Copy, ["bk%d" % (m % 2)], ["NB%d" % m], scale=-1.0)
 
-    def sign(m, a, b, k):
-        o = 512 * ROWS[k] - (384 if k == 3 else 0)
-        act(T.SG[:, C * m + a:C * m + b], T.PS[:, o + a:o + b], F.Sign, ["bk%d" % ROWS[k], "NB%d" % m], runs("SG%d" % m, a, b, 128),
+    def sign(m, a, b, bank):
+        o = 512 * bank - first[bank]
+        act(T.SG[:, C * m + a:C * m + b], T.PS[:, o + a:o + b], F.Sign, ["bk%d" % bank, "NB%d" % m], runs("SG%d" % m, a, b, 128),
             bias=T.NB[:, 10 * m + 9:10 * m + 10])
-
-    def signs(k, straight):
-        negs(k)
-        if k == 3:
-            sign(1, 256, 384, 2)
-            sign(3, 0, 384, 2)
-            sign(3, 384, C, 3)
-            return
-        if k:
-            sign(0, 128 * k, 128 * k + 128, k)
-        sign(k, 128 * k if straight else 0, 128 * k + 128, k)
 
     def runmin(a, b):
         scan(T.RUN[:, 10 * a:10 * b], T.RS[:, 10 * a:10 * b], T.NB[:, 10 * a:10 * b], 0.0, A.add, A.min,
@@ -234,56 +265,61 @@ def rank_program(g, core, T, topo):
     def before(m, a, b):
         o = C * m
         rd, wr = runs("SG%d" % m, a, b, 128), runs("CM%d" % m, a, b, 128)
-        if a == 128 * m:
+        if a == 128 * m and m not in HALVED:
             tt(T.CM[:, o + a:o + b], T.SG[:, o + a:o + b], T.THR[:, 0:b - a], A.is_gt, rd + ["THR"], wr)
         else:
             ts(T.CM[:, o + a:o + b], T.SG[:, o + a:o + b], 0.0, None, [A.is_ge if a < 128 * m else A.is_gt], rd, wr)
 
-    def last_run(m):
-        ts(T.CM[:, C * m + 384:C * m + C], T.PS[:, 1024:1088], T.NB[:, 10 * m + 9:10 * m + 10], 0.0, [A.add, A.is_gt],
-           ["bk2", "NB%d" % m], ["CM%d.3" % m])
+    def direct(m, a, b, bank):
+        o = 512 * bank - first[bank]
+        ts(T.CM[:, C * m + a:C * m + b], T.PS[:, o + a:o + b], T.NB[:, 10 * m + 9:10 * m + 10], 0.0, [A.add, A.is_ge if a < 128 * m else A.is_gt],
+           ["bk%d" % bank, "NB%d" % m], runs("CM%d" % m, a, b, 128))
 
     def count(m):
         o = C * m
-        scan(T.SCN[:, 224 * m:224 * m + 224], T.CM[:, o:o + 224], T.CM[:, o + 224:o + C], -225.0, A.add, A.add,
-             runs("CM%d" % m, 0, C, 128), ["SCN%d" % m])
+        scan(T.SCN[:, 224 * m:224 * m + 224], T.CM[:, o:o + 224], T.CM[:, o + 224:o + C], T.IN[:, m:m + 1] if m in HALVED else -225.0,
+             A.add, A.add, runs("CM%d" % m, 0, C, 128) + (["IN%d" % m] if m in HALVED else []), ["SCN%d" % m])
 
-    def scores_tail(straight):
-        if straight:
-            ts(T.CM[:, 2 * C:2 * C + 256], T.PS[:, 1536:1792], T.NB[:, 29:30], 0.0, [A.add, A.is_ge], ["bk3", "NB2"], runs("CM2", 0, 256, 128))
-        before(0, 128, 384)
-        last_run(0); last_run(1); last_run(2)
-        count(0)
-        if not straight:
-            before(2, 0, 256)
-        before(2, 256, 384)
-        runmin(2, 4)
-        level(2); level(3)
-        before(1, 256, 384)
-        count(2)
+    def lower(m):
+        do("g", g.affine_select, (T.TRI[:, 128 * m:128 * m + 128], T.SG[:, (C + 128) * m:(C + 128) * m + 128], [[-1, 128]], A.is_ge, 0.0, 0, 1),
+           ["SG%d.%d" % (m, m)], ["TRI%d" % m])
+
+    def equal(m):
+        act(T.TRJ[:, :], T.TRI[:, 128 * m:128 * m + 128], F.Abs, ["TRI%d" % m], ["TRJ", "WA%d" % m], accum_out=T.WA[:, m:m + 1])
+        act(T.IN[:, m:m + 1], T.WA[:, m:m + 1], F.Identity, ["WA%d" % m, "PF"], ["IN%d" % m], bias=T.PF[:, 0:1], scale=-1.0)
+
+    def calls():
         ts(T.CF[:, :], T.NB[:, 8:40:10], 0.0, 16.0, [A.is_lt, A.mult], ["NB0", "NB1", "NB2", "NB3"], ["CF"])
-        before(3, 0, 384)
-        before(3, 384, C)
-        count(1)
-        count(3)
-        tt(T.SCN[:, 4 * 224 + 223:1792:224], T.CF[:, :], T.LV[:, :], A.subtract, ["LV0", "LV1", "LV2", "LV3", "CF"], ["SCNw"])
 
-    LRK = ["LRe0", "LRe1", "LR1", "LR2", "LR3"]
-    RKK = ["RK%d" % b for b in range(4)]
+    def kinds():
+        tt(T.SCN[:, 4 * 224 + 223:1792:224], T.CF[:, :], T.LV[:, :], A.subtract, ["LV0", "LV1", "LV2", "LV3", "CF", "SCNy"], ["SCNw"])
 
-    def lists():
-        rd = ["SCN0", "SCN1", "SCN2", "SCN3", "SCNw"]
-        for b in range(1, 4):
-            move("vvs"[b - 1], T.SCN[0:32, 223 + 56 * b:1968:224], T.SCN[32 * b:32 * b + 32, 223:1792:224], rd, ["NAT%d" % b])
-        do("v", V.transpose, (T.TT[0:32, 0:32], T.SCN[0:32, 223:1968:56]), rd + ["NAT1", "NAT2", "NAT3"], ["TT"])
-        for e in range(2):
-            move("vs"[e], T["LT%d" % e][:, :], T.TT[:, 0:32].indirect(T["DUP%d" % e][:, 0:2]), ["TT", "DUP%d" % e], ["LT%d" % e])
-        for e in range(2):
-            do("v", V.transpose, (T.LR[0:32, e:64:2], T["LT%d" % e][0:32, 0:32]), ["LT%d" % e], ["LRe%d" % e])
+    OWN = ["SCN0", "SCN1", "SCN2", "SCN3", "SCNw", "SCNz"]
+    LRK = OWN + ["AG%d" % b for b in range(6)] + ["LB%d" % b for b in range(4)] + ["LK", "LC"]
+    RKK = ["RK"]
+
+    def lists(t):
+        def between(i):
+            if t == 0:
+                places(i)
+
+        between(6)
+        for b in range(5):
+            do("v", V.transpose, (T.TT[0:32, 32 * b:32 * b + 32], T.SCN[32 * (b % 4):32 * (b % 4) + 32, 223:7168:224]), OWN, ["TT%d" % b])
+        between(7)
+        for b in range(2):
+            act(T.SCN[64 * b:64 * b + 64, 111:1792:224], T.SCN[64 - 64 * b:128 - 64 * b, 223:1792:224], F.Copy, OWN, ["AG%d" % b])
         for b in range(4):
-            ts(T.RK[32 * b:32 * b + 32, :], T.LR[0:32, 0:28], 224.0, None, [A.add], ["LRe0", "LRe1"], ["RK%d" % b])
-        for b in range(1, 4):
-            act(T.LR[32 * b:32 * b + 32, 0:64], T.LR[0:32, 0:64], F.Copy, ["LRe0", "LRe1"], ["LR%d" % b])
+            do("v", V.transpose, (T.SCN[32 * b:32 * b + 32, 1792:1920], T.TT[0:32, 16:144]), ["TT%d" % i for i in range(5)], ["LB%d" % b])
+        for b in range(4):
+            a = 32 * ((b + 1) % 4)
+            act(T.SCN[32 * b:32 * b + 32, 55:1792:112], T.SCN[a:a + 32, 111:1792:112], F.Copy, OWN + ["AG0", "AG1"], ["AG%d" % (2 + b)])
+        between(8)
+        ts(T.RK[:, :], spread("LK"), 224.0, None, [A.add], LRK, RKK)
+        between(9)
+
+    def spread(name):
+        return T.SCN[:, 0:1920].indirect(T[name][:, 0:2])
 
     def sort(win, t, a, b, key):
         vcopy(win.indirect(T.RK[:, a // 16:b // 16]), row(t, a, b), RKK + runs("DR%d" % t, a, b), [key])
@@ -296,22 +332,19 @@ def rank_program(g, core, T, topo):
 
     def pointers(t):
         d, s = C * (t + 1), C * (t + 2)
-        act(T.y1[:, :], T.LR[:, 32:60], F.Abs, LRK + ["NG"], ["y1"], bias=T.NG[:, 0:1])
-        act(T.r1[:, :], T.LR[:, 0:28], F.Identity, LRK, ["r1"], bias=225.0 + s + C)
+        act(T.y1[:, :], spread("LC"), F.Abs, LRK + ["NG"], ["y1"], bias=T.NG[:, 0:1])
+        act(T.MB[:, 0:128:4], spread("LK"), F.Identity, LRK, ["r1"], bias=225.0 + s + C)
         act(T.y2[:, :], T.y1[:, :], F.Abs, ["y1"], ["y2"], bias=-(d + 15 * s) / 2, scale=float(s))
-        act(T.wf[:, :], T.LR[:, 0:28], F.Relu, LRK, ["wf"], bias=-222.0 * C, scale=float(C))
-        act(T.y3[:, :], T.y2[:, :], F.Relu, ["y2"], ["y3"], bias=-(15 * s - d) / 2)
+        act(T.MB[:, 1:128:4], spread("LK"), F.Identity, LRK, ["r2"], bias=223.0 * 1024 + s + C, scale=-1024.0)
+        act(T.MB[:, 2:128:4], T.y2[:, :], F.Relu, ["y2"], ["y3"], bias=-(15 * s - d) / 2)
         if t == 0:
             act(T.TB[:, TP:TP + C], row(0), F.Copy, runs("DR0", 0, C), ["P0"])
-            act(T.MASK[:, :], T.YO[:, :], F.Identity, ["YO"], ["MASK"], bias=-8192.0)
+            act(T.MASK[:, :], T.YO[:, :], F.Identity, ["YO"], ["MASK"], bias=-3840.0, scale=4352.0)
         sort(T.TB[:, TS:TS + C], t, 0, 288, "TBs")
-        tt(T.o1[:, :], T.y3[:, :], T.JW[:, :], A.add, ["y3", "JW"], ["o1"])
-        tt(T.lm[:, :], T.r1[:, :], T.wf[:, :], A.subtract, ["r1", "wf"], ["lm"])
-        sort(T.TB[:, TS:TS + C], t, 288, 384, "TBs")
-        tt(T.o2[:, :], T.o1[:, :], T.lm[:, :], A.min, ["o1", "lm"], ["o2"])
-        sort(T.TB[:, TS:TS + C], t, 384, C, "TBs")
-        vcopy(T.OL[:, :], T.o2[:, :], ["o2"], ["OL"])
-        ts(T.RK1[:, :], T.lm[:, :], -float(s + C), None, [A.add], ["lm"], ["RK1"])
+        scan(T.MO[:, :], T.MA[:, :], T.MB[:, :], 0.0, A.add, A.min, ["MA0", "MA1", "MA2", "MA3", "MB", "r1", "r2", "y3"], ["MO"])
+        sort(T.TB[:, TS:TS + C], t, 288, C, "TBs")
+        vcopy(T.OL[:, :], T.MO[:, 3:128:4], ["MO"], ["OL"])
+        ts(T.RK1[:, :], T.MO[:, 1:128:4], -float(s + C), None, [A.add], ["MO"], ["RK1"])
 
     def pick(qn, t, a, b):
         rd = ["TBs", "OL", "IO", "P0"] + [k for i in range(t + 1) for k in runs("DR%d" % i, 0, C)]
@@ -323,11 +356,16 @@ def rank_program(g, core, T, topo):
         rid, pid, _ = topo.addr(dst)
         m = topo.mask(core, dst)
         waits("g", ["QZ%dh%d" % (t, h)], [])
+        part = 1
+        masks = [m, m]
+        if t == h == 0:
+            part = 2
+            masks = [sum(1 << e for e in topo.engines(core, dst)[i::2]) for i in range(2)]
         g.remote_dma(T["LZ%d" % t][:, a:b].bitcast(dt.uint8), T["QZ%d" % t][:, a:b].bitcast(dt.uint8),
-                     T.sem["ar%d%d" % (t, h)], T.sem.loc, pid, rid, m)
-        g.remote_dma(T["LZS%d" % t][:, a:b], T["QZS%d" % t][:, a:b], T.sem["ar%d%d" % (t, h)], T.sem.loc, pid, rid, m)
-        cnt["loc"] = cnt.get("loc", 0) + 2 * len(topo.engines(core, dst))
-        lastw["LZ%dh%d" % (t, h)] = ("ar%d%d" % (t, h), 2 * len(topo.engines(T.cores[(rank - 1 - t) % N], core)), None)
+                     T.sem["ar%d%d" % (t, h)], T.sem.loc, pid, rid, masks[0])
+        g.remote_dma(T["LZS%d" % t][:, a:b], T["QZS%d" % t][:, a:b], T.sem["ar%d%d" % (t, h)], T.sem.loc, pid, rid, masks[1])
+        cnt["loc"] = cnt.get("loc", 0) + 2 * len(topo.engines(core, dst)) // part
+        lastw["LZ%dh%d" % (t, h)] = ("ar%d%d" % (t, h), 2 * len(topo.engines(T.cores[(rank - 1 - t) % N], core)) // part, None)
 
     def mosaic(t):
         def part(qn, a, b):
@@ -352,12 +390,10 @@ def rank_program(g, core, T, topo):
 
     def join_list(t):
         sort(T.PD[:, 0:C], t + 1, 0, C, "PD")
-        layer(t, 0)
-        for h, qn in enumerate("vs"):
-            a, b = 224 * h, 224 * h + 224
-            move(qn, T.VR[:, a:b], T.PD[:, 0:C].indirect(T.RK1[:, a // 16:b // 16]), ["PD", "RK1"], runs("VR", a, b))
-        for h in range(2):
-            a, b = 224 * h, 224 * h + 224
+        halves = ((0, 224), (224, C))
+        for a, b in halves:
+            vcopy(T.VR[:, a:b], T.PD[:, 0:C].indirect(T.RK1[:, a // 16:b // 16]), ["PD", "RK1"], runs("VR", a, b))
+        for a, b in halves:
             fold(T.VR[:, a:b], runs("VR", a, b), a, b)
         four("EL", 0, 224)
 
@@ -385,83 +421,60 @@ def rank_program(g, core, T, topo):
         act(T.JG[:, 0:4 * (b - a)], T.HS[:, 0:4 * C].indirect(T.EL[:, a // 4:b // 4]), F.Copy, HK + runs("EL", a, b), ["JG"])
         dma("g", "ga%d" % t, T.X[:, 4 * a:4 * b], T.JG[:, 0:4 * (b - a)], ["JG"] + runs("X", a, b), runs("X", a, b), accum_op=A.add)
 
-    def score(m, straight=False):
-        quant_x(m)
-        products(m, straight)
-        signs(m, straight)
+    def first_pointers():
+        vcopy(T.PL[:, :], T.PI[:, :], ["PI"], ["PL"])
+
+    step = {"join": join, "quant": quant_x, "cols": cols, "line": line, "negs": negs, "sign": sign, "before": before, "direct": direct,
+            "runmin": runmin, "level": level, "count": count, "calls": calls, "kinds": kinds, "places": places, "lower": lower, "equal": equal, "late": late_constants, "first": first_pointers}
+
+    def scores(order):
+        for c in order:
+            step[c[0]](*c[1:])
 
     quant(T.QU[:, :], T.QUS[:, :], T.UT[:, :], ["UT"], ["QU"])
+    places(0)
     vcopy(T.QU1[:, :].bitcast(dt.uint32), T.QU[:, 0:128].bitcast(dt.uint32).indirect(T.U1L[:, 0:9]), ["QU", "U1L"], ["QU1c"])
     act(T.QU1S[:, :], T.QUS[:, 0:128].indirect(T.U1L[:, 0:9]), F.Copy, ["QU", "U1L"], ["QU1s"])
-    score(0)
-    late_constants()
-    score(1)
-    vcopy(T.PL[:, :], T.PI[:, :], ["PI"], ["PL"])
-    before(0, 0, 128)
-    runmin(0, 2)
-    level(0); level(1)
-    score(2, True)
-    score(3)
-    before(1, 0, 128)
-    before(1, 128, 256)
-    scores_tail(True)
+    scores(START)
     act(row(0), T.TB[:, TI:TI + C].indirect(T.PL[:, 0:28]), F.Copy, ["IO", "PL"], runs("DR0", 0, C))
 
     def result(a, b):
-        m = a // 128
-        quant(T.QX[:, a:b], T.QXS[:, a:b], T.X[:, 4 * a:4 * b], runs("X", a, b), runs("QX", a, b, 128))
-        if b > 128:
-            lo = a if b == C else 0
-            dma("y", "sto%d" % (4 + m), T.oc[:, 4 * lo:4 * b], T.QX[:, lo:b].bitcast(dt.uint8), runs("QX", lo, b, 128), ["oc%d" % m])
-        mm(m, b - a, T.QV[:, :], T.QVS[:, :], T.QX[:, a:b], T.QXS[:, a:b], ["QV"] + runs("QX", a, b, 128))
-        move("v" if b == C else "s", T.YS[:, a:b], T.PS[:, 512 * m:512 * m + b - a], ["bk%d" % m], runs("YS", a, b, 128))
+        m = a // 160
+        quant(T.QX[:, a:b], T.QXS[:, a:b], T.X[:, 4 * a:4 * b], runs("X", a, b), runs("QX", a, b))
+        dma("y", "sto%d" % (4 + m), T.oc[:, 4 * a:4 * b], T.QX[:, a:b].bitcast(dt.uint8), runs("QX", a, b), ["oc%d" % m])
+        mm(m, b - a, T.QV[:, :], T.QVS[:, :], T.QX[:, a:b], T.QXS[:, a:b], ["QV"] + runs("QX", a, b))
+        move("v" if b == C else "s", T.YS[:, a:b], T.PS[:, 512 * m:512 * m + b - a], ["bk%d" % m], runs("YS", a, b))
 
     def store(qn, i, a, b):
-        dma(qn, "sto%d" % i, T.y[:, a:b], T.YS[:, a:b], runs("YS", a, b, 128), ["y%d" % i])
+        dma(qn, "sto%d" % i, T.y[:, a:b], T.YS[:, a:b], runs("YS", a, b), ["y%d" % i])
 
     for t in range(R):
-        lists()
+        lists(t)
         pointers(t)
         mosaic(t)
         join_list(t)
         if t == 0:
             quant(T.QV[:, :], T.QVS[:, :], T.VT[:, :], ["VT"], ["QV"])
-        for h in range(1, len(ZP)):
+        for h in range(len(ZP)):
             layer(t, h)
         four("EL", 224, C)
         if t == R - 1:
             act(T.YO[:, :], row(R), F.Identity, runs("DR%d" % R, 0, C), ["YO"], bias=float(MID))
             dma("y", "sto0", T.op[:, :], T.YO[0:128:16, :], ["YO"], ["op"])
         if t < R - 1:
-            join(0, 128)
-            join(128, 160)
-            score(0)
-            join(160, 256)
-            join(256, 288)
-            score(1)
-            join(288, JD)
-            before(0, 0, 128)
-            quant_x(2)
-            runmin(0, 2)
-            level(0); level(1)
-            products(2, True)
-            signs(2, True)
-            join(JD, C)
-            before(1, 0, 128)
-            score(3)
-            before(1, 128, 256)
-            scores_tail(True)
-    join(0, 128)
-    join(128, 256)
-    result(0, 128)
-    join(256, 352)
-    result(128, 256)
-    store("y", 1, 0, 256)
-    join(352, C)
-    result(256, C)
+            scores(JOIN)
+    join(0, 160)
+    join(160, 320)
+    result(0, 160)
+    store("s", 1, 0, 160)
+    join(320, 384)
+    result(160, 320)
+    store("s", 2, 160, 320)
+    join(384, C)
+    result(320, C)
     for k in range(4):
-        dma("s" if k > 1 else "y", "sto%d" % (8 + k), T.osc[4 * k:4 * k + 4, :], T.QXS[32 * k:32 * k + 4, 0:C], runs("QX", 0, C, 128), ["osc%d" % k])
-    store("s", 2, 256, C)
+        dma("s" if k > 1 else "y", "sto%d" % (8 + k), T.osc[4 * k:4 * k + 4, :], T.QXS[32 * k:32 * k + 4, 0:C], runs("QX", 0, C), ["osc%d" % k])
+    store("y", 3, 320, C)
     kn = known["g"]
     for s in sorted(cnt):
         if kn.get(s, 0) < cnt[s]:

@@ -3,23 +3,26 @@ from concourse.mybir import dt, AluOpType as A, ActivationFunctionType as F
 C, R, N = 448, 3, 4
 MID = 224
 ZP = [(0, 128), (128, 304), (304, 448)]
-MOSAIC = [("pick", "v", 0, 64), ("pick", "s", 64, 128), ("pick", "v", 128, 224), ("pick", "s", 224, 448),
-          ("fold", 0, 128), ("fold", 128, 224), ("four", 0, 128), ("part", "s", 64, 128), ("four", 128, 224), ("part", "v", 0, 64),
-          ("fold", 224, 448), ("part", "s", 128, 224), ("pack", 0), ("four", 224, 448), ("part", "s", 352, 448), ("part", "v", 224, 304),
-          ("pack", 1), ("part", "v", 304, 352), ("pack", 2)]
-TAIL = [("direct", 2, 0, 256, 3), ("before", 0, 128, 384), ("direct", 0, 384, C, 2), ("direct", 1, 384, C, 2), ("direct", 2, 384, C, 2), ("count", 0),
-        ("before", 2, 256, 384), ("runmin", 2, 4), ("level", 2), ("level", 3), ("before", 1, 256, 384), ("count", 2), ("calls",),
-        ("before", 3, 0, 384), ("before", 3, 384, C), ("count", 1), ("count", 3), ("kinds",)]
-RUN0 = [("quant", 0), ("cols", 0), ("line", 4, 0, 128), ("negs", 0), ("sign", 0, 0, 128, 4)]
-RUN1 = [("quant", 1), ("cols", 1), ("line", 5, 0, 256), ("line", 3, 0, 256), ("negs", 1), ("sign", 0, 128, 256, 5), ("sign", 1, 0, 256, 5)]
-RUN2 = [("cols", 2), ("line", 6, 256, 384), ("negs", 2), ("sign", 0, 256, 384, 6), ("sign", 2, 256, 384, 6)]
-RUN3 = [("quant", 3), ("cols", 3), ("line", 2, 384, 512), ("line", 7, 256, C), ("negs", 3), ("sign", 1, 256, 384, 6), ("sign", 3, 0, 256, 5), ("sign", 3, 256, C, 7)]
-START = (RUN0 + [("places", 1), ("late",)] + RUN1
-         + [("places", 2), ("first",), ("places", 5), ("places", 3), ("before", 0, 0, 128), ("places", 4), ("runmin", 0, 2), ("level", 0), ("level", 1), ("quant", 2)]
-         + RUN2 + RUN3 + [("before", 1, 0, 128), ("before", 1, 128, 256)] + TAIL)
-JOIN = ([("join", 0, 128), ("join", 128, 160)] + RUN0 + [("join", 160, 256), ("join", 256, 288)] + RUN1
-        + [("join", 288, 384), ("before", 0, 0, 128), ("quant", 2), ("runmin", 0, 2), ("level", 0), ("level", 1)] + RUN2
-        + [("join", 384, C), ("before", 1, 0, 128)] + RUN3 + [("before", 1, 128, 256)] + TAIL)
+MOSAIC = [("pick", "s", 64, 128), ("pick", "s", 224, C), ("pick", "v", 0, 64), ("pick", "v", 128, 224),
+          ("fold", 0, 128), ("fold", 128, 224), ("four", 0, 128), ("fold", 224, C), ("four", 128, 224),
+          ("part", "s", 64, 128), ("part", "v", 0, 64), ("four", 224, C), ("pack", 0),
+          ("part", "s", 128, 224), ("part", "s", 352, C), ("part", "v", 224, 304), ("part", "v", 304, 352), ("pack", 1), ("pack", 2)]
+START = [("quant", 0), ("cols", 0), ("line", 4, 0, 128), ("first",), ("places", 1), ("quant", 1), ("places", 2), ("quant", 2), ("places", 5),
+         ("cols", 1), ("negs", 0), ("late",), ("quant", 3), ("sign", 0, 0, 128, 4), ("line", 5, 0, 256), ("cols", 2), ("negs", 1), ("before", 0, 0, 128),
+         ("line", 6, 256, 384), ("line", 3, 0, 256), ("sign", 0, 128, 256, 5), ("cols", 3), ("runmin", 0, 2), ("negs", 2), ("line", 2, 384, 512),
+         ("sign", 1, 0, 256, 5), ("places", 3), ("line", 7, 256, C), ("direct", 2, 0, 256, 3), ("negs", 3), ("sign", 1, 256, 384, 6),
+         ("direct", 1, 384, C, 2), ("sign", 0, 256, 384, 6), ("sign", 2, 256, 384, 6), ("direct", 0, 384, C, 2), ("sign", 3, 256, C, 7),
+         ("before", 1, 128, 256), ("places", 4), ("runmin", 2, 4), ("before", 1, 256, 384), ("before", 0, 128, 384), ("before", 1, 0, 128),
+         ("sign", 3, 0, 256, 5), ("direct", 2, 384, C, 2), ("before", 2, 256, 384), ("calls",), ("level", 2), ("count", 0), ("count", 1), ("level", 0),
+         ("before", 3, 0, 384), ("before", 3, 384, C), ("level", 3), ("level", 1), ("count", 2), ("kinds",), ("count", 3)]
+JOIN = [("join", 0, 256), ("join", 256, 304), ("quant", 0), ("quant", 1), ("cols", 0), ("cols", 1), ("line", 5, 0, 256), ("negs", 0), ("negs", 1),
+        ("join", 304, 384), ("line", 3, 0, 256), ("sign", 1, 0, 256, 5), ("join", 384, C), ("sign", 0, 0, 256, 5),
+        ("quant", 2), ("cols", 2), ("runmin", 0, 2), ("line", 6, 256, 384), ("level", 0), ("negs", 2),
+        ("quant", 3), ("before", 1, 128, 256), ("before", 1, 0, 128), ("sign", 0, 256, 384, 6), ("cols", 3), ("line", 2, 384, 512), ("before", 0, 0, 128),
+        ("negs", 3), ("line", 7, 256, C), ("sign", 2, 256, 384, 6), ("direct", 2, 0, 256, 3), ("sign", 1, 256, 384, 6), ("sign", 3, 256, C, 7),
+        ("direct", 0, 384, C, 2), ("direct", 2, 384, C, 2), ("before", 0, 128, 384), ("before", 2, 256, 384), ("calls",), ("before", 1, 256, 384),
+        ("sign", 3, 0, 256, 5), ("level", 1), ("direct", 1, 384, C, 2), ("runmin", 2, 4), ("count", 2), ("level", 3), ("count", 0),
+        ("before", 3, 384, C), ("before", 3, 0, 384), ("level", 2), ("count", 1), ("kinds",), ("count", 3)]
 HALVED = []
 XL = [(0, 128), (128, 256), (256, 448)]
 JD = 384
@@ -157,7 +160,7 @@ def rank_program(g, core, T, topo):
         kw = {"allow_small_or_imprecise_dtypes": True} if flag else {}
         do("g", g.iota, (out, pattern, base, mult), [], [key], **kw)
 
-    def runs(name, a, b, n=32):
+    def runs(name, a, b, n=16):
         return ["%s.%d" % (name, i) for i in range(a // n, (b - 1) // n + 1)]
 
     def row(t, a=0, b=C):
@@ -390,12 +393,12 @@ def rank_program(g, core, T, topo):
 
     def join_list(t):
         sort(T.PD[:, 0:C], t + 1, 0, C, "PD")
-        halves = ((0, 224), (224, C))
+        halves = ((0, 256), (256, C))
         for a, b in halves:
             vcopy(T.VR[:, a:b], T.PD[:, 0:C].indirect(T.RK1[:, a // 16:b // 16]), ["PD", "RK1"], runs("VR", a, b))
         for a, b in halves:
             fold(T.VR[:, a:b], runs("VR", a, b), a, b)
-        four("EL", 0, 224)
+        four("EL", 0, 256)
 
     def layer(t, h):
         a, b = ZP[h]
@@ -406,7 +409,7 @@ def rank_program(g, core, T, topo):
         for w in range(4):
             bk = 4 * (h % 2) + w
             o, i, rd, wr = T.HS[:, 4 * a + w:4 * b:4], T.PS[:, 512 * bk:512 * bk + b - a], ["bk%d" % bk], ["HS%dh%d" % (w, h)]
-            if last and w % 2:
+            if (last and w % 2) or (h == 1 and w == 3):
                 ts(o, i, 0.00390625, None, [A.mult], rd, wr)
             else:
                 act(o, i, F.Copy, rd, wr, scale=0.00390625)
@@ -443,7 +446,8 @@ def rank_program(g, core, T, topo):
         quant(T.QX[:, a:b], T.QXS[:, a:b], T.X[:, 4 * a:4 * b], runs("X", a, b), runs("QX", a, b))
         dma("y", "sto%d" % (4 + m), T.oc[:, 4 * a:4 * b], T.QX[:, a:b].bitcast(dt.uint8), runs("QX", a, b), ["oc%d" % m])
         mm(m, b - a, T.QV[:, :], T.QVS[:, :], T.QX[:, a:b], T.QXS[:, a:b], ["QV"] + runs("QX", a, b))
-        move("v" if b == C else "s", T.YS[:, a:b], T.PS[:, 512 * m:512 * m + b - a], ["bk%d" % m], runs("YS", a, b))
+        if a == 0:
+            act(T.YS[:, a:b], T.PS[:, 0:b], F.Copy, ["bk0"], runs("YS", a, b))
 
     def store(qn, i, a, b):
         dma(qn, "sto%d" % i, T.y[:, a:b], T.YS[:, a:b], runs("YS", a, b), ["y%d" % i])
@@ -457,23 +461,24 @@ def rank_program(g, core, T, topo):
             quant(T.QV[:, :], T.QVS[:, :], T.VT[:, :], ["VT"], ["QV"])
         for h in range(len(ZP)):
             layer(t, h)
-        four("EL", 224, C)
+        four("EL", 256, C)
         if t == R - 1:
             act(T.YO[:, :], row(R), F.Identity, runs("DR%d" % R, 0, C), ["YO"], bias=float(MID))
             dma("y", "sto0", T.op[:, :], T.YO[0:128:16, :], ["YO"], ["op"])
         if t < R - 1:
             scores(JOIN)
-    join(0, 160)
-    join(160, 320)
-    result(0, 160)
-    store("s", 1, 0, 160)
-    join(320, 384)
-    result(160, 320)
-    store("s", 2, 160, 320)
-    join(384, C)
+    join(0, 192)
+    join(192, 320)
+    result(0, 192)
+    store("s", 1, 0, 192)
+    join(320, C)
+    result(192, 320)
     result(320, C)
     for k in range(4):
         dma("s" if k > 1 else "y", "sto%d" % (8 + k), T.osc[4 * k:4 * k + 4, :], T.QXS[32 * k:32 * k + 4, 0:C], runs("QX", 0, C), ["osc%d" % k])
+    for a, b in ((192, 320), (320, C)):
+        vcopy(T.YS[:, a:b], T.PS[:, 512 * (a // 160):512 * (a // 160) + b - a], ["bk%d" % (a // 160)], runs("YS", a, b))
+    store("s", 2, 192, 320)
     store("y", 3, 320, C)
     kn = known["g"]
     for s in sorted(cnt):

from concourse.mybir import dt, AluOpType as A, ActivationFunctionType as F

C, R, N = 448, 3, 4
MID = 224
ZP = [(0, 128), (128, 304), (304, 448)]
MOSAIC = [("pick", "s", 64, 128), ("pick", "s", 224, C), ("pick", "v", 0, 64), ("pick", "v", 128, 224),
          ("fold", 0, 128), ("fold", 128, 224), ("four", 0, 128), ("fold", 224, C), ("four", 128, 224),
          ("part", "s", 64, 128), ("part", "v", 0, 64), ("four", 224, C), ("pack", 0),
          ("part", "s", 128, 224), ("part", "s", 352, C), ("part", "v", 224, 304), ("part", "v", 304, 352), ("pack", 1), ("pack", 2)]
START = [("quant", 0), ("cols", 0), ("line", 4, 0, 128), ("first",), ("places", 1), ("quant", 1), ("places", 2), ("quant", 2), ("places", 5),
         ("cols", 1), ("negs", 0), ("late",), ("quant", 3), ("sign", 0, 0, 128, 4), ("line", 5, 0, 256), ("cols", 2), ("negs", 1), ("before", 0, 0, 128),
         ("line", 6, 256, 384), ("line", 3, 0, 256), ("sign", 0, 128, 256, 5), ("cols", 3), ("runmin", 0, 2), ("negs", 2), ("line", 2, 384, 512),
         ("sign", 1, 0, 256, 5), ("places", 3), ("line", 7, 256, C), ("direct", 2, 0, 256, 3), ("negs", 3), ("sign", 1, 256, 384, 6),
         ("direct", 1, 384, C, 2), ("sign", 0, 256, 384, 6), ("sign", 2, 256, 384, 6), ("direct", 0, 384, C, 2), ("sign", 3, 256, C, 7),
         ("before", 1, 128, 256), ("places", 4), ("runmin", 2, 4), ("before", 1, 256, 384), ("before", 0, 128, 384), ("before", 1, 0, 128),
         ("sign", 3, 0, 256, 5), ("direct", 2, 384, C, 2), ("before", 2, 256, 384), ("calls",), ("level", 2), ("count", 0), ("count", 1), ("level", 0),
         ("before", 3, 0, 384), ("before", 3, 384, C), ("level", 3), ("level", 1), ("count", 2), ("kinds",), ("count", 3)]
JOIN = [("join", 0, 256), ("join", 256, 304), ("quant", 0), ("quant", 1), ("cols", 0), ("cols", 1), ("line", 5, 0, 256), ("negs", 0), ("negs", 1),
        ("join", 304, 384), ("line", 3, 0, 256), ("sign", 1, 0, 256, 5), ("join", 384, C), ("sign", 0, 0, 256, 5),
        ("quant", 2), ("cols", 2), ("runmin", 0, 2), ("line", 6, 256, 384), ("level", 0), ("negs", 2),
        ("quant", 3), ("before", 1, 128, 256), ("before", 1, 0, 128), ("sign", 0, 256, 384, 6), ("cols", 3), ("line", 2, 384, 512), ("before", 0, 0, 128),
        ("negs", 3), ("line", 7, 256, C), ("sign", 2, 256, 384, 6), ("direct", 2, 0, 256, 3), ("sign", 1, 256, 384, 6), ("sign", 3, 256, C, 7),
        ("direct", 0, 384, C, 2), ("direct", 2, 384, C, 2), ("before", 0, 128, 384), ("before", 2, 256, 384), ("calls",), ("before", 1, 256, 384),
        ("sign", 3, 0, 256, 5), ("level", 1), ("direct", 1, 384, C, 2), ("runmin", 2, 4), ("count", 2), ("level", 3), ("count", 0),
        ("before", 3, 384, C), ("before", 3, 0, 384), ("level", 2), ("count", 1), ("kinds",), ("count", 3)]
HALVED = []
XL = [(0, 128), (128, 256), (256, 448)]
JD = 384
BIG = 1.0e29
TP, TI, TS = 4 * C, 5 * C, 6 * C


def _b(n, t="float32"):
    return ("sbuf", [128, n], t)


BF, CODE, U8, U16, I32 = "bfloat16", "float8_e4m3fn_x4", "uint8", "uint16", "int32"
SCRATCH = {
    "PS": ("psum", [128, 4096], "float32"),
    "X": _b(2048, BF), "JG": _b(4 * (C - JD)), "UT": _b(512, BF), "VT": _b(512, BF), "Z": _b(1792, BF), "THR": _b(128, BF),
    "SG": _b(1792, BF), "CM": _b(1792, BF), "SCN": _b(7168, BF),
    "TRI": _b(384, BF), "TRJ": _b(128, BF), "WA": _b(3), "IN": _b(3), "TT": _b(160, BF),
    "QU": _b(128, CODE), "QUS": _b(128, U8), "QU1": _b(144, CODE), "QU1S": _b(144, U8), "QV": _b(128, CODE), "QVS": _b(128, U8),
    "WC": _b(512, CODE), "WS": _b(512, U8), "QX": _b(512, CODE), "QXS": _b(512, U8),
    "PI": _b(28, I32), "PIX": _b(1, I32), "PMI": _b(1, I32), "GI": _b(1, I32), "PQI": _b(1, I32), "PEI": _b(1, I32),
    "Q2I": _b(1, I32), "H2I": _b(1, I32), "Q2": _b(1), "H2": _b(1), "LK": _b(2, U16), "LC": _b(2, U16), "PL": _b(28, U16), "U1L": _b(10, U16), "OF": _b(112, U16), "EL": _b(112, U16),
    "TB": _b(7 * C, BF), "PD": _b(448, BF), "VR": _b(448, BF), "SC": _b(448, "float16"), "MASK": _b(448, BF),
    "MD": _b(448), "HS": _b(1792), "YS": _b(448), "YO": _b(448),
    "NB": _b(40), "RS": _b(40), "RUN": _b(40), "LJ": _b(32), "LV": _b(4), "CF": _b(4),
}
for _i in ("PM", "PF", "NG", "PQ", "PE", "PO", "u1", "u2", "u3"):
    SCRATCH[_i] = _b(1)
for _i in ("RK", "RK1", "OL"):
    SCRATCH[_i] = _b(32, U16)
for _i in ("A16", "JW", "y1", "y2"):
    SCRATCH[_i] = _b(32)
for _i in ("MA", "MB", "MO"):
    SCRATCH[_i] = _b(128)
for _i in ("k0", "k1", "k2", "km", "kd", "kb", "ke"):
    SCRATCH[_i] = _b(2, I32)
for _i in ("c1", "c2", "c3", "cs", "ca", "cb", "cd", "ce", "cp", "c4", "cc"):
    SCRATCH[_i] = _b(2)
for _i in range(R):
    for _n in ("QZ", "LZ"):
        SCRATCH["%s%d" % (_n, _i)] = _b(448, CODE)
        SCRATCH["%sS%d" % (_n, _i)] = _b(448, U8)

SEMAPHORES = ["sv", "ss", "st", "sg", "loc"]
SEMAPHORES += ["ld%d" % _i for _i in range(8)] + ["ga%d" % _i for _i in range(R - 1)] + ["sto%d" % _i for _i in range(12)]
SEMAPHORES += ["ar%d%d" % (_t, _h) for _t in range(R) for _h in range(len(ZP))]


def rank_program(g, core, T, topo):
    rank = T.rank_of(core)
    if rank is None:
        return
    q = {"v": g.vector, "s": g.scalar, "t": g.tensor, "g": g, "y": g.sync}
    own = {"v": "sv", "s": "ss", "t": "st", "g": "sg"}
    cnt, known, clock, lastw, readers = {}, {k: {} for k in q}, {}, {}, {}

    def waits(qn, reads, writes):
        need = {}
        for k in reads:
            if k in lastw:
                s, n, _ = lastw[k]
                need[s] = max(need.get(s, 0), n)
        for k in writes:
            if k in lastw:
                s, n, _ = lastw[k]
                need[s] = max(need.get(s, 0), n)
            for s, n, rq in readers.get(k, []):
                if rq != qn:
                    need[s] = max(need.get(s, 0), n)
        kn = known[qn]
        need = {s: n for s, n in need.items() if kn.get(s, 0) < n}
        for s in list(need):
            if any(o != s and clock.get((o, need[o]), {}).get(s, 0) >= need[s] for o in need):
                del need[s]
        for s, n in need.items():
            q[qn].wait_ge(T.sem[s], n)
            for o, m in clock.get((s, n), {}).items():
                kn[o] = max(kn.get(o, 0), m)
            kn[s] = max(kn.get(s, 0), n)

    def note(qn, reads, writes, s, n, dma):
        clock[(s, n)] = dict(known[qn])
        for k in writes:
            lastw[k] = (s, n, qn)
            readers[k] = []
        for k in reads:
            readers.setdefault(k, []).append((s, n, None if dma else qn))

    def do(qn, fn, args, reads, writes, **kw):
        waits(qn, reads, writes)
        s = own[qn]
        n = cnt.get(s, 0) + 1
        cnt[s] = n
        fn(*args, **kw).then_inc(T.sem[s], 1)
        note(qn, reads, writes, s, n, False)

    def dma(qn, s, out, in_, reads, writes, **kw):
        waits(qn, reads, writes)
        q[qn].dma_start(out, in_, **kw).then_inc(T.sem[s], 16)
        cnt[s] = 16
        note(qn, reads, writes, s, 16, True)

    V, S, TE = g.vector, g.scalar, g.tensor

    def ts(out, in0, s1, s2, ops, reads, writes):
        do("v", V.tensor_scalar, (out, in0, s1, s2) + tuple(ops), reads, writes)

    def tt(out, a, b, op, reads, writes):
        do("v", V.tensor_tensor, (out, a, b, op), reads, writes)

    def vcopy(out, a, reads, writes):
        do("v", V.tensor_copy, (out, a), reads, writes)

    def act(out, a, f, reads, writes, **kw):
        do("s", S.activation, (out, a, f), reads, writes, **kw)

    def move(qn, out, a, reads, writes):
        if qn == "v":
            vcopy(out, a, reads, writes)
        else:
            act(out, a, F.Copy, reads, writes)

    def scan(out, a, b, init, o0, o1, reads, writes):
        do("v", V.tensor_tensor_scan, (out, a, b, init, o0, o1), reads, writes)

    def quant(oc, os_, tile, reads, writes):
        do("v", V.quantize_mx, (oc, os_, tile), reads, writes)

    def mm(bank, n, l, ls, r, rs, reads):
        do("t", TE.matmul_mx, (T.PS[:, 512 * bank:512 * bank + n], l, ls, r, rs, True, True), reads, ["bk%d" % bank])

    def fill(ap, c, key):
        do("v", V.memset, (ap, c), [], [key])

    def iota(out, pattern, key, mult=0, flag=True, base=0):
        kw = {"allow_small_or_imprecise_dtypes": True} if flag else {}
        do("g", g.iota, (out, pattern, base, mult), [], [key], **kw)

    def runs(name, a, b, n=16):
        return ["%s.%d" % (name, i) for i in range(a // n, (b - 1) // n + 1)]

    def row(t, a=0, b=C):
        return T.TB[:, (R - t) * C + a:(R - t) * C + b]

    dma("s", "ld0", T.UT[:, :], T.u[:, :], [], ["UT"])
    for i, (a, b) in enumerate(XL):
        dma("y", "ld%d" % (1 + i), T.X[:, 4 * a:4 * b], T.x[:, 4 * a:4 * b], [], runs("X", a, b))
    dma("s", "ld4", T.PI[:, :], T.p[:, :], [], ["PI"])
    waits("y", runs("X", 0, C), [])
    dma("y", "ld5", T.WC[:, :].bitcast(dt.uint8), T.wc[:, :], [], ["WC"])
    dma("y", "ld6", T.WS[:, :], T.ws[:, :], [], ["WS"])
    dma("y", "ld7", T.VT[:, :], T.v[:, :], [], ["VT"])

    iota(T.PIX[:, :], [[0, 1]], "PIX", 1, False)
    iota(T.A16[:, :], [[16, 32]], "A16")
    iota(T.MD[:, :], [[0, 112], [1, 4]], "MD")
    iota(T.TB[:, TI:TI + C], [[1, C]], "IO", base=-MID)
    iota(T.SCN[:, 896:1792], [[0, 896]], "SCNy")
    fill(T.U1L[:, :], 1, "U1L")
    do("v", V.memset, (T.X[:, 4 * C:2048], 0.0), [], runs("X", C, 512))
    fill(T.RS[:, :], 0.0, "RS")

    def c1(o, a, s1, s2, *ops):
        col = [s for s in (s1, s2) if s in SCRATCH]
        n = SCRATCH[o][1][1]
        ts(T[o][:, 0:n], T[a][:, 0:n], T[s1][:, 0:1] if s1 in col else s1, T[s2][:, 0:1] if s2 in col else s2, ops, [a] + col, [o])

    def c2(o, a, b, op):
        tt(T[o][:, :], T[a][:, :], T[b][:, :], op, [a, b], [o])

    SHR, AND = A.arith_shift_right, A.bitwise_and
    c1("PMI", "PIX", 15, None, AND); c1("PQI", "PIX", 2, 3, SHR, AND); c1("Q2I", "PIX", 4, 6, SHR, AND); c1("H2I", "PIX", 3, 2, SHR, AND)
    c1("PM", "PMI", 0.0, None, A.add); c1("u1", "PMI", 16.0, -1.0, A.mult, A.add); c1("PQ", "PQI", -1.0, -0.5, A.mult, A.add); c1("PF", "PIX", -float(MID), None, A.add)
    c1("u2", "PM", 8.0, "u1", A.is_lt, A.mult); c1("JW", "A16", "PM", None, A.add); c1("Q2", "Q2I", 0.0, None, A.add); c1("H2", "H2I", 0.0, None, A.add)
    c1("u3", "PM", 8.0, "u2", A.is_equal, A.add)
    c1("k0", "JW", 0.0, None, A.add); c1("k1", "JW", "Q2", 8.0, A.subtract, A.add); c1("k2", "JW", "H2", 8.0, A.subtract, A.add)
    ts(T.U1L[:, 0:1], T.u3[:, :], 1.0, None, [A.add], ["u3", "U1L"], ["U1L"])
    c1("km", "k0", 3, None, SHR); c1("ke", "k0", 1, None, AND); c1("kd", "k1", 1, 3, SHR, AND); c1("kb", "k2", 1, 3, SHR, AND)
    fill(T.RS[:, 0:40:10], BIG, "RS")
    c1("c1", "km", 224.0, 223.0, A.mult, A.add); c1("c2", "kd", -56.0, None, A.mult)
    c1("c3", "kb", 32.0, 1792.0, A.mult, A.add); c1("cs", "ke", 2.0, "H2", A.mult, A.is_equal)
    act(T.YO[:, :], T.MD[:, :], F.Sign, ["MD", "PQ"], ["YO"], bias=T.PQ[:, 0:1])

    def late_constants():
        ts(T.THR[:, :], T.TB[:, TI:TI + 128], T.PF[:, 0:1], 0.5, [A.is_gt, A.subtract], ["IO", "PF"], ["THR"])

    def places(i):
        if i == 0:
            c2("ca", "c1", "c2", A.add); c2("cb", "c3", "km", A.add)
        elif i == 1:
            c2("cd", "ca", "cb", A.subtract); c1("c4", "cs", 892.0, 4.0, A.mult, A.add)
        elif i == 2:
            c2("ce", "cd", "cs", A.mult)
        elif i == 3:
            c2("cp", "cb", "ce", A.add)
        elif i == 4:
            c2("cc", "cp", "c4", A.add)
        elif i == 5:
            fill(T.SCN[:, 2015:7168:224], 0.0, "SCNz")
        elif i == 6:
            c1("LK", "cp", 0.0, None, A.add); c1("LC", "cc", 0.0, None, A.add); c1("GI", "PIX", 4, None, SHR)
        elif i == 7:
            c1("NG", "GI", -1.0, None, A.mult); c1("PEI", "PIX", 3, None, AND)
            fill(T.MB[:, 3:128:4], 65536.0, "MB")
        elif i == 8:
            fill(T.MA[:, 0:128:4], 65536.0, "MA0"); fill(T.MA[:, 1:128:4], 0.0, "MA1")
            c1("u1", "PQI", 2048.0, 4.0 * MID - 3 * 2048, A.mult, A.add)
        else:
            ts(T.MA[:, 2:128:4], T.JW[:, :], -1.0, None, [A.mult], ["JW"], ["MA2"]); vcopy(T.MA[:, 3:128:4], T.JW[:, :], ["JW"], ["MA3"])
            c1("PO", "PEI", "u1", None, A.add)

    def quant_x(m):
        a = 128 * m
        quant(T.QX[:, a:a + 128], T.QXS[:, a:a + 128], T.X[:, 4 * a:4 * a + 512], runs("X", a, a + 128), ["QX.%d" % m])

    UK = ["QU1c", "QU1s"]

    first = {}

    def cols(m):
        a = 128 * m
        mm(m % 2, 128, T.QX[:, a:a + 128], T.QXS[:, a:a + 128], T.QU1[:, 0:128], T.QU1S[:, 0:128], ["QX.%d" % m] + UK)

    def line(bank, a, b):
        first[bank] = a
        mm(bank, b - a, T.QU1[:, 16:144], T.QU1S[:, 16:144], T.QX[:, a:b], T.QXS[:, a:b], runs("QX", a, b, 128) + UK)

    def negs(m):
        act(T.NB[:, 10 * m:10 * m + 10], T.PS[:, 512 * (m % 2):512 * (m % 2) + 10], F.Copy, ["bk%d" % (m % 2)], ["NB%d" % m], scale=-1.0)

    def sign(m, a, b, bank):
        o = 512 * bank - first[bank]
        act(T.SG[:, C * m + a:C * m + b], T.PS[:, o + a:o + b], F.Sign, ["bk%d" % bank, "NB%d" % m], runs("SG%d" % m, a, b, 128),
            bias=T.NB[:, 10 * m + 9:10 * m + 10])

    def runmin(a, b):
        scan(T.RUN[:, 10 * a:10 * b], T.RS[:, 10 * a:10 * b], T.NB[:, 10 * a:10 * b], 0.0, A.add, A.min,
             ["RS"] + ["NB%d" % m for m in range(a, b)], ["RUN%d" % m for m in range(a, b)])

    def level(m):
        act(T.LJ[:, 8 * m:8 * m + 8], T.RUN[:, 10 * m:10 * m + 8], F.Sign, ["RUN%d" % m], ["LJ%d" % m, "LV%d" % m],
            bias=T.RUN[:, 10 * m + 7:10 * m + 8], scale=-1.0, accum_out=T.LV[:, m:m + 1])

    def before(m, a, b):
        o = C * m
        rd, wr = runs("SG%d" % m, a, b, 128), runs("CM%d" % m, a, b, 128)
        if a == 128 * m and m not in HALVED:
            tt(T.CM[:, o + a:o + b], T.SG[:, o + a:o + b], T.THR[:, 0:b - a], A.is_gt, rd + ["THR"], wr)
        else:
            ts(T.CM[:, o + a:o + b], T.SG[:, o + a:o + b], 0.0, None, [A.is_ge if a < 128 * m else A.is_gt], rd, wr)

    def direct(m, a, b, bank):
        o = 512 * bank - first[bank]
        ts(T.CM[:, C * m + a:C * m + b], T.PS[:, o + a:o + b], T.NB[:, 10 * m + 9:10 * m + 10], 0.0, [A.add, A.is_ge if a < 128 * m else A.is_gt],
           ["bk%d" % bank, "NB%d" % m], runs("CM%d" % m, a, b, 128))

    def count(m):
        o = C * m
        scan(T.SCN[:, 224 * m:224 * m + 224], T.CM[:, o:o + 224], T.CM[:, o + 224:o + C], T.IN[:, m:m + 1] if m in HALVED else -225.0,
             A.add, A.add, runs("CM%d" % m, 0, C, 128) + (["IN%d" % m] if m in HALVED else []), ["SCN%d" % m])

    def lower(m):
        do("g", g.affine_select, (T.TRI[:, 128 * m:128 * m + 128], T.SG[:, (C + 128) * m:(C + 128) * m + 128], [[-1, 128]], A.is_ge, 0.0, 0, 1),
           ["SG%d.%d" % (m, m)], ["TRI%d" % m])

    def equal(m):
        act(T.TRJ[:, :], T.TRI[:, 128 * m:128 * m + 128], F.Abs, ["TRI%d" % m], ["TRJ", "WA%d" % m], accum_out=T.WA[:, m:m + 1])
        act(T.IN[:, m:m + 1], T.WA[:, m:m + 1], F.Identity, ["WA%d" % m, "PF"], ["IN%d" % m], bias=T.PF[:, 0:1], scale=-1.0)

    def calls():
        ts(T.CF[:, :], T.NB[:, 8:40:10], 0.0, 16.0, [A.is_lt, A.mult], ["NB0", "NB1", "NB2", "NB3"], ["CF"])

    def kinds():
        tt(T.SCN[:, 4 * 224 + 223:1792:224], T.CF[:, :], T.LV[:, :], A.subtract, ["LV0", "LV1", "LV2", "LV3", "CF", "SCNy"], ["SCNw"])

    OWN = ["SCN0", "SCN1", "SCN2", "SCN3", "SCNw", "SCNz"]
    LRK = OWN + ["AG%d" % b for b in range(6)] + ["LB%d" % b for b in range(4)] + ["LK", "LC"]
    RKK = ["RK"]

    def lists(t):
        def between(i):
            if t == 0:
                places(i)

        between(6)
        for b in range(5):
            do("v", V.transpose, (T.TT[0:32, 32 * b:32 * b + 32], T.SCN[32 * (b % 4):32 * (b % 4) + 32, 223:7168:224]), OWN, ["TT%d" % b])
        between(7)
        for b in range(2):
            act(T.SCN[64 * b:64 * b + 64, 111:1792:224], T.SCN[64 - 64 * b:128 - 64 * b, 223:1792:224], F.Copy, OWN, ["AG%d" % b])
        for b in range(4):
            do("v", V.transpose, (T.SCN[32 * b:32 * b + 32, 1792:1920], T.TT[0:32, 16:144]), ["TT%d" % i for i in range(5)], ["LB%d" % b])
        for b in range(4):
            a = 32 * ((b + 1) % 4)
            act(T.SCN[32 * b:32 * b + 32, 55:1792:112], T.SCN[a:a + 32, 111:1792:112], F.Copy, OWN + ["AG0", "AG1"], ["AG%d" % (2 + b)])
        between(8)
        ts(T.RK[:, :], spread("LK"), 224.0, None, [A.add], LRK, RKK)
        between(9)

    def spread(name):
        return T.SCN[:, 0:1920].indirect(T[name][:, 0:2])

    def sort(win, t, a, b, key):
        vcopy(win.indirect(T.RK[:, a // 16:b // 16]), row(t, a, b), RKK + runs("DR%d" % t, a, b), [key])

    def fold(src, keys, a, b):
        scan(T.SC[:, a:b], T.MASK[:, a:b], src, 0.0, A.add, A.max, ["MASK"] + keys, runs("SC", a, b))

    def four(name, a, b):
        ts(T[name][:, a // 4:b // 4], T.SC[:, a + 3:b:4], 4.0, T.PO[:, 0:1], [A.mult, A.add], runs("SC", a, b) + ["PO"], runs(name, a, b))

    def pointers(t):
        d, s = C * (t + 1), C * (t + 2)
        act(T.y1[:, :], spread("LC"), F.Abs, LRK + ["NG"], ["y1"], bias=T.NG[:, 0:1])
        act(T.MB[:, 0:128:4], spread("LK"), F.Identity, LRK, ["r1"], bias=225.0 + s + C)
        act(T.y2[:, :], T.y1[:, :], F.Abs, ["y1"], ["y2"], bias=-(d + 15 * s) / 2, scale=float(s))
        act(T.MB[:, 1:128:4], spread("LK"), F.Identity, LRK, ["r2"], bias=223.0 * 1024 + s + C, scale=-1024.0)
        act(T.MB[:, 2:128:4], T.y2[:, :], F.Relu, ["y2"], ["y3"], bias=-(15 * s - d) / 2)
        if t == 0:
            act(T.TB[:, TP:TP + C], row(0), F.Copy, runs("DR0", 0, C), ["P0"])
            act(T.MASK[:, :], T.YO[:, :], F.Identity, ["YO"], ["MASK"], bias=-3840.0, scale=4352.0)
        sort(T.TB[:, TS:TS + C], t, 0, 288, "TBs")
        scan(T.MO[:, :], T.MA[:, :], T.MB[:, :], 0.0, A.add, A.min, ["MA0", "MA1", "MA2", "MA3", "MB", "r1", "r2", "y3"], ["MO"])
        sort(T.TB[:, TS:TS + C], t, 288, C, "TBs")
        vcopy(T.OL[:, :], T.MO[:, 3:128:4], ["MO"], ["OL"])
        ts(T.RK1[:, :], T.MO[:, 1:128:4], -float(s + C), None, [A.add], ["MO"], ["RK1"])

    def pick(qn, t, a, b):
        rd = ["TBs", "OL", "IO", "P0"] + [k for i in range(t + 1) for k in runs("DR%d" % i, 0, C)]
        move(qn, row(t + 1, a, b), T.TB[:, (R - t) * C:7 * C].indirect(T.OL[:, a // 16:b // 16]), rd, runs("DR%d" % (t + 1), a, b))

    def send(t, h):
        a, b = ZP[h]
        dst = T.cores[(rank + 1 + t) % N]
        rid, pid, _ = topo.addr(dst)
        m = topo.mask(core, dst)
        waits("g", ["QZ%dh%d" % (t, h)], [])
        part = 1
        masks = [m, m]
        if t == h == 0:
            part = 2
            masks = [sum(1 << e for e in topo.engines(core, dst)[i::2]) for i in range(2)]
        g.remote_dma(T["LZ%d" % t][:, a:b].bitcast(dt.uint8), T["QZ%d" % t][:, a:b].bitcast(dt.uint8),
                     T.sem["ar%d%d" % (t, h)], T.sem.loc, pid, rid, masks[0])
        g.remote_dma(T["LZS%d" % t][:, a:b], T["QZS%d" % t][:, a:b], T.sem["ar%d%d" % (t, h)], T.sem.loc, pid, rid, masks[1])
        cnt["loc"] = cnt.get("loc", 0) + 2 * len(topo.engines(core, dst)) // part
        lastw["LZ%dh%d" % (t, h)] = ("ar%d%d" % (t, h), 2 * len(topo.engines(T.cores[(rank - 1 - t) % N], core)) // part, None)

    def mosaic(t):
        def part(qn, a, b):
            move(qn, T.Z[:, 4 * a:4 * b], T.X[:, 0:4 * C].indirect(T.OF[:, a // 4:b // 4]), runs("X", 0, C) + runs("OF", a, b), runs("Z", a, b, 8))

        def pack(h):
            a, b = ZP[h]
            quant(T["QZ%d" % t][:, a:b], T["QZS%d" % t][:, a:b], T.Z[:, 4 * a:4 * b], runs("Z", a, b, 8), ["QZ%dh%d" % (t, h)])
            send(t, h)

        for c in MOSAIC:
            if c[0] == "pick":
                pick(c[1], t, c[2], c[3])
            elif c[0] == "fold":
                fold(row(t + 1, c[1], c[2]), runs("DR%d" % (t + 1), c[1], c[2]), c[1], c[2])
            elif c[0] == "four":
                four("OF", c[1], c[2])
            elif c[0] == "part":
                part(*c[1:])
            else:
                pack(c[1])

    def join_list(t):
        sort(T.PD[:, 0:C], t + 1, 0, C, "PD")
        halves = ((0, 256), (256, C))
        for a, b in halves:
            vcopy(T.VR[:, a:b], T.PD[:, 0:C].indirect(T.RK1[:, a // 16:b // 16]), ["PD", "RK1"], runs("VR", a, b))
        for a, b in halves:
            fold(T.VR[:, a:b], runs("VR", a, b), a, b)
        four("EL", 0, 256)

    def layer(t, h):
        a, b = ZP[h]
        last = h == len(ZP) - 1
        for w in range(4):
            mm(4 * (h % 2) + w, b - a, T.WC[:, 128 * w:128 * w + 128], T.WS[:, 128 * w:128 * w + 128], T["LZ%d" % t][:, a:b], T["LZS%d" % t][:, a:b],
               ["WC", "WS", "LZ%dh%d" % (t, h)])
        for w in range(4):
            bk = 4 * (h % 2) + w
            o, i, rd, wr = T.HS[:, 4 * a + w:4 * b:4], T.PS[:, 512 * bk:512 * bk + b - a], ["bk%d" % bk], ["HS%dh%d" % (w, h)]
            if (last and w % 2) or (h == 1 and w == 3):
                ts(o, i, 0.00390625, None, [A.mult], rd, wr)
            else:
                act(o, i, F.Copy, rd, wr, scale=0.00390625)

    HK = ["HS%dh%d" % (w, h) for w in range(4) for h in range(len(ZP))]

    def join(a, b):
        tt(T.X[:, 4 * a:4 * b], T.HS[:, 0:4 * C].indirect(T.EL[:, a // 4:b // 4]), T.X[:, 4 * a:4 * b], A.add,
           HK + runs("EL", a, b) + runs("X", a, b), runs("X", a, b))

    def join_by_dma(t, a, b):
        act(T.JG[:, 0:4 * (b - a)], T.HS[:, 0:4 * C].indirect(T.EL[:, a // 4:b // 4]), F.Copy, HK + runs("EL", a, b), ["JG"])
        dma("g", "ga%d" % t, T.X[:, 4 * a:4 * b], T.JG[:, 0:4 * (b - a)], ["JG"] + runs("X", a, b), runs("X", a, b), accum_op=A.add)

    def first_pointers():
        vcopy(T.PL[:, :], T.PI[:, :], ["PI"], ["PL"])

    step = {"join": join, "quant": quant_x, "cols": cols, "line": line, "negs": negs, "sign": sign, "before": before, "direct": direct,
            "runmin": runmin, "level": level, "count": count, "calls": calls, "kinds": kinds, "places": places, "lower": lower, "equal": equal, "late": late_constants, "first": first_pointers}

    def scores(order):
        for c in order:
            step[c[0]](*c[1:])

    quant(T.QU[:, :], T.QUS[:, :], T.UT[:, :], ["UT"], ["QU"])
    places(0)
    vcopy(T.QU1[:, :].bitcast(dt.uint32), T.QU[:, 0:128].bitcast(dt.uint32).indirect(T.U1L[:, 0:9]), ["QU", "U1L"], ["QU1c"])
    act(T.QU1S[:, :], T.QUS[:, 0:128].indirect(T.U1L[:, 0:9]), F.Copy, ["QU", "U1L"], ["QU1s"])
    scores(START)
    act(row(0), T.TB[:, TI:TI + C].indirect(T.PL[:, 0:28]), F.Copy, ["IO", "PL"], runs("DR0", 0, C))

    def result(a, b):
        m = a // 160
        quant(T.QX[:, a:b], T.QXS[:, a:b], T.X[:, 4 * a:4 * b], runs("X", a, b), runs("QX", a, b))
        dma("y", "sto%d" % (4 + m), T.oc[:, 4 * a:4 * b], T.QX[:, a:b].bitcast(dt.uint8), runs("QX", a, b), ["oc%d" % m])
        mm(m, b - a, T.QV[:, :], T.QVS[:, :], T.QX[:, a:b], T.QXS[:, a:b], ["QV"] + runs("QX", a, b))
        if a == 0:
            act(T.YS[:, a:b], T.PS[:, 0:b], F.Copy, ["bk0"], runs("YS", a, b))

    def store(qn, i, a, b):
        dma(qn, "sto%d" % i, T.y[:, a:b], T.YS[:, a:b], runs("YS", a, b), ["y%d" % i])

    for t in range(R):
        lists(t)
        pointers(t)
        mosaic(t)
        join_list(t)
        if t == 0:
            quant(T.QV[:, :], T.QVS[:, :], T.VT[:, :], ["VT"], ["QV"])
        for h in range(len(ZP)):
            layer(t, h)
        four("EL", 256, C)
        if t == R - 1:
            act(T.YO[:, :], row(R), F.Identity, runs("DR%d" % R, 0, C), ["YO"], bias=float(MID))
            dma("y", "sto0", T.op[:, :], T.YO[0:128:16, :], ["YO"], ["op"])
        if t < R - 1:
            scores(JOIN)
    join(0, 192)
    join(192, 320)
    result(0, 192)
    store("s", 1, 0, 192)
    join(320, C)
    result(192, 320)
    result(320, C)
    for k in range(4):
        dma("s" if k > 1 else "y", "sto%d" % (8 + k), T.osc[4 * k:4 * k + 4, :], T.QXS[32 * k:32 * k + 4, 0:C], runs("QX", 0, C), ["osc%d" % k])
    for a, b in ((192, 320), (320, C)):
        vcopy(T.YS[:, a:b], T.PS[:, 512 * (a // 160):512 * (a // 160) + b - a], ["bk%d" % (a // 160)], runs("YS", a, b))
    store("s", 2, 192, 320)
    store("y", 3, 320, C)
    kn = known["g"]
    for s in sorted(cnt):
        if kn.get(s, 0) < cnt[s]:
            g.wait_ge(T.sem[s], cnt[s])
